import numpy as np, ml_dtypes
CORES = [36,164,52,180,100,228,116,244]
N = 8
BF = ml_dtypes.bfloat16
W, C, B, VI, S = 3072, 2048, 128, 3, 5
def parts(rng):
    rt = rng.integers(0, 16, (N, 8, 16, W)); pf = rng.integers(0, W, (N, 8, 16, C))
    jc = np.argsort(rng.random((N, 8, C)), axis=-1)[..., :16 * B].reshape(N, 8, 16, B)
    return rt, pf, jc, rng.integers(0, 16, (N, 8, 16, B)), rng.integers(0, 16, (N, 8, B))
def pack(rt, pf, jc, fx, sr):
    return {"rt": np.ascontiguousarray(rt.reshape(N, 128, W)).astype(np.float32).astype(BF),
            "pk": np.ascontiguousarray((pf[..., :C // 2] + 4096 * pf[..., C // 2:]).reshape(N, 128, C // 2)).astype(np.int32),
            "jc": np.ascontiguousarray(jc.reshape(N, 128, B)).astype(np.int32),
            "fx": np.ascontiguousarray(fx.reshape(N, 128, B)).astype(np.float32).astype(BF), "sr": np.ascontiguousarray(sr).astype(np.int32)}
def setup_inputs(rng):
    return pack(*parts(rng))
def setup_inputs_ties(rng):
    rt, pf, jc, fx, sr = parts(rng)
    pool = rng.integers(0, 16, (N, 8, 16, 8)); pool[:, 1::2] = rng.integers(0, 2, (N, 4, 16, 8))
    rt = np.take_along_axis(pool, rng.integers(0, 8, (N, 8, 1, W)), 3)
    fx = np.where(rng.random((N, 8, 1, B)) < 0.5, np.take_along_axis(pool, rng.integers(0, 8, (N, 8, 1, B)), 3), fx)
    q = rng.permutation(C)[:C // 8]; pf[..., q] = pf[:, :, :1, q]
    return pack(rt, pf, jc, fx, sr)
def setup_inputs_rounds(rng):
    rt, pf, jc, fx, sr = parts(rng); h = W // 2
    o = np.argsort(rng.random((N, 8, W)), axis=-1); light = np.zeros((N, 8, W), bool); np.put_along_axis(light, o[..., :h], True, 2)
    rt = np.where(light[:, :, None, :], rng.integers(0, 2, (N, 8, 16, W)), rng.integers(8, 16, (N, 8, 16, W)))
    ln = rng.integers(1, S + 2, (8, B)); back = (rng.random((8, B)) * ln).astype(np.int64)
    ln[0] = S; back[0] = 0; ln[1] = S + 1; ln[2] = 1; back[2] = 0
    if np.count_nonzero(ln <= S) % 2 == 0:
        ln[3, 0] = S + 1 if ln[3, 0] <= S else S; back[3, 0] = 0
    s0 = rng.integers(0, 16, (8, B)); a = (np.arange(16)[None, :, None] - s0[:, None, :]) % 16
    nxt = (np.where(a == ln[:, None, :] - 1, back[:, None, :], a + 1) + s0[:, None, :]) % 16
    pc = np.argsort(rng.random((8, C)), axis=-1)[:, :16 * B]
    kap = rng.integers(0, 16, (8, C)); np.put_along_axis(kap, pc, nxt.reshape(8, 16 * B), 1)
    one = kap[None, :, None, :] == np.arange(16)[None, None, :, None]
    pf = np.take_along_axis(o[:, :, None, :], rng.integers(0, h, (N, 8, 16, C)) + np.where(one, 0, h), 3)
    e = np.argsort(rng.random((N, 8, B)), axis=-1)
    jc = np.take_along_axis(np.broadcast_to(pc.reshape(1, 8, 16, B), (N, 8, 16, B)), np.broadcast_to(e[:, :, None, :], (N, 8, 16, B)), 3)
    sr = np.take_along_axis(np.broadcast_to(s0[None], (N, 8, B)), e, 2)
    return pack(rt, pf, jc, rng.integers(0, 2, (N, 8, 16, B)), sr)
def setup_inputs_full(rng):
    h = W // 2; u = h // 2; rows = np.arange(16)
    side = (np.arange(N)[:, None] + np.arange(8)[None, :]) % 2 * h
    o = np.argsort(rng.random((N, 8, h)), axis=-1) + side[:, :, None]; light = np.zeros((N, 8, W), bool); np.put_along_axis(light, o[..., :u], True, 2)
    rt = np.where(light[:, :, None, :], rng.integers(0, 2, (N, 8, 16, W)), rng.integers(8, 16, (N, 8, 16, W)))
    s0 = 2 * rng.permutation(8) + rng.integers(0, 2, 8); a = (rows[None, :] - s0[:, None]) % 16
    nxt = (np.where(a == S - 1, 0, a + 1) + s0[:, None]) % 16
    lower = np.argsort(rng.random((8, C // 2)), axis=-1)[:, :8 * B]; upper = np.argsort(rng.random((8, C // 2)), axis=-1)[:, :8 * B] + C // 2
    pc = np.concatenate([lower, upper], axis=1).reshape(8, 16, B)
    kap = rng.integers(0, 16, (N, 8, C))
    np.put_along_axis(kap, np.broadcast_to(pc.reshape(1, 8, 16 * B), (N, 8, 16 * B)), np.broadcast_to(np.repeat(nxt, B, axis=1)[None], (N, 8, 16 * B)), 2)
    whole = int(rng.integers(0, 8))
    for g in range(8):
        if g != whole: kap[1::2, g, int(pc[g, (s0[g] + S - 1) % 16, 0])] = (s0[g] + S) % 16
    one = kap[:, :, None, :] == rows[None, None, :, None]
    pf = np.take_along_axis(o[:, :, None, :], rng.integers(0, u, (N, 8, 16, C)) + np.where(one, 0, u), 3)
    e = np.argsort(rng.random((N, 8, 16, B)), axis=-1)
    jc = np.take_along_axis(np.broadcast_to(pc[None], (N, 8, 16, B)), e, 3)
    return pack(rt, pf, jc, rng.integers(0, 2, (N, 8, 16, B)), np.broadcast_to(s0[None, :, None], (N, 8, B)))
def setup_inputs_ends(rng):
    rt, pf, jc, fx, sr = parts(rng)
    pf[:, ::2] = rng.choice(np.array([0, 1, W // 2, W - 1]), (N, 4, 16, C)); pf[:, 1::2, :, C // 2 - 1] = W - 1; pf[:, 1::2, :, C - 1] = W - 1
    jc[:, ::2] = np.concatenate([np.arange(8 * B), np.arange(C - 8 * B, C)]).reshape(16, B)
    rt[:, 1::2] = 15 * rng.integers(0, 2, (N, 4, 16, W)); fx = 15 * rng.integers(0, 2, (N, 8, 16, B)); sr = 15 * rng.integers(0, 2, (N, 8, B))
    o = rng.permutation(W); n = B // 2; hi = o[:W // 4]; mid = o[W // 4:W // 2]; lo = o[W // 2:3 * W // 4]
    rt[:, 1][:, :, hi] = 15; rt[:, 1][:, :, mid] = 14; rt[:, 1][:, :, lo] = 0
    for q in range(N):
        x = rng.permutation(B)[:n]; p = np.argsort(rng.random((16, n)), axis=0)[:3]; c = jc[q, 1, p, x]
        for i, k, a, b in ((0, p[1], mid, hi), (1, p[2], hi, lo), (2, p[1], lo, hi)):
            pf[q, 1][:, c[i]] = rng.choice(b, (16, n)); pf[q, 1][k, c[i]] = rng.choice(a, n)
        fx[q, 1][:, x] = 0; sr[q, 1][x] = p[0]
    return pack(rt, pf, jc, fx, sr)
def setup_inputs_spread(rng):
    rt, pf, jc, fx, sr = parts(rng)
    rt = np.minimum((16 * rng.random((N, 8, 16, W)) ** np.exp2(rng.integers(-2, 4, (N, 8, 1, W)))).astype(np.int64), 15)
    pf = np.minimum((W * rng.random((N, 8, 16, C)) ** np.exp2(rng.integers(-2, 4, (N, 8, 1, C)))).astype(np.int64), W - 1)
    fx = np.minimum((16 * rng.random((N, 8, 16, B)) ** np.exp2(rng.integers(-2, 4, (N, 8, 1, B)))).astype(np.int64), 15)
    sr = np.minimum((16 * rng.random((N, 8, B)) ** np.exp2(rng.integers(-1, 3, (N, 8, 1)))).astype(np.int64), 15)
    return pack(rt, pf, jc, fx, sr)
def check_inputs(d):
    bad = []
    for k in ("rt", "fx"):
        a = np.asarray(d[k]).astype(np.float32)
        if not np.all((a >= 0) & (a <= 15) & (a == np.floor(a))): bad.append("whole numbers of " + k)
    a = np.asarray(d["pk"]).astype(np.int64)
    if np.min(a) < 0 or np.max(a & 4095) >= W or np.max(a >> 12) >= W: bad.append("range of pk")
    for k, hi in (("jc", C - 1), ("sr", 15)):
        if np.min(d[k]) < 0 or np.max(d[k]) > hi: bad.append("range of " + k)
    s = np.sort(np.asarray(d["jc"]).reshape(N, 8, 16 * B), axis=-1)
    if np.any(s[..., 1:] == s[..., :-1]): bad.append("courts of a group differ")
    return bad
def reference(rt, pk, jc, fx, sr):
    R = rt.astype(np.float32).astype(np.int32).reshape(N, 8, 16, W); f = fx.astype(np.float32).astype(np.int32).reshape(N, 8, 16, B)
    two = pk.astype(np.int32).reshape(N, 8, 16, C // 2); pf = np.concatenate([two & 4095, two >> 12], axis=3)
    J = jc.astype(np.int32).reshape(N, 8, 16, B); start = sr.astype(np.int32); Z = np.zeros(N, np.int32); rows = np.arange(16, dtype=np.int32)
    for t in range(VI):
        if t > 0:
            f = np.roll(f, 1, axis=0); J = np.roll(J, 1, axis=0); start = np.roll(start, 1, axis=0)
        m = np.zeros((N, 8, 16, B), np.int32); v = np.zeros((N, 8, 16, B), np.int32); num = np.zeros((N, 8, 16, B), np.int32)
        p = start; go = np.ones((N, 8, B), bool); first = np.zeros((N, 8, B), np.int32); new = np.zeros((N, 8, B), np.int32)
        for s in range(1, S + 1):
            c = np.take_along_axis(J, p[:, :, None, :], 2)
            n = np.take_along_axis(pf, np.broadcast_to(c, (N, 8, 16, B)), 3)
            x = np.take_along_axis(R, np.broadcast_to(n.reshape(N, 8, 1, 16 * B), (N, 8, 16, 16 * B)), 3).reshape(N, 8, 16, 16, B)
            dist = np.add.reduce(np.abs(x - f[:, :, :, None, :]), axis=2)
            k = np.argmin(dist, axis=2).astype(np.int32)
            kk = k[:, :, None, :]; nk = np.take_along_axis(n, kk, 2)
            rule = np.take_along_axis(R, np.broadcast_to(nk, (N, 8, 16, B)), 3)
            here = (rows[None, None, :, None] == p[:, :, None, :]) & go[:, :, None, :]
            v = np.where(here, kk, v); num = np.where(here, nk, num); m = np.where(here, np.int32(s), m)
            f = np.where(go[:, :, None, :], np.abs(f - rule), f)
            mk = np.take_along_axis(m, kk, 2)[:, :, 0]; nr = np.take_along_axis(num, kk, 2)
            shut = go & (mk > 0)
            tot = np.add.reduce(np.take_along_axis(R, np.broadcast_to(nr, (N, 8, 16, B)), 3), axis=2)
            odd = ((tot + Z[:, None, None]) & 1) == 1
            new = np.where(shut, np.where(odd, nk[:, :, 0], nr[:, :, 0]), new); first = np.where(shut, mk, first)
            go = go & ~shut; p = np.where(go, k, p)
        closed = first > 0
        loop = closed[:, :, None, :] & (m >= first[:, :, None, :])
        at = np.broadcast_to(J.reshape(N, 8, 1, 16 * B), (N, 8, 16, 16 * B))
        old = np.take_along_axis(pf, at, 3).reshape(N, 8, 16, 16, B)
        hit = loop[:, :, None] & (v[:, :, None] == rows[None, None, :, None, None])
        np.put_along_axis(pf, at, np.where(hit, new[:, :, None, None, :], old).reshape(N, 8, 16, 16 * B), 3)
        Z = Z + np.add.reduce(closed.astype(np.int32), axis=(1, 2))
    return {"yp": (pf[..., :C // 2] + 4096 * pf[..., C // 2:]).reshape(N, 128, C // 2).astype(np.float32), "yf": f.reshape(N, 128, B).astype(np.float32).astype(BF)}

@@ -1,0 +1,410 @@
+from concourse.mybir import AluOpType, AxisListType, ActivationFunctionType
+
+A = AluOpType
+AF = ActivationFunctionType
+VI, S = 3, 5
+NDUM = 640
+SCRATCH = {}
+for _n, _s, _d in (
+        ("pkt tmpi", [128, 1024], "int32"), ("rtt", [128, 3072], "bfloat16"), ("tab", [128, 2048 + NDUM], "float32"),
+        ("jci jh jl", [128, 128], "int32"), ("sri", [8, 128], "int32"), ("srb bo8", [8, 128], "bfloat16"),
+        ("fin0 fin1 fin2 fout oneb idb idn jhb jlb oh", [128, 128], "bfloat16"), ("fw0 fw1 fw2", [128, 272], "bfloat16"),
+        ("pi yli", [128, 1], "int32"), ("ylf y16 q2k zr zc", [128, 1], "float32"),
+        ("io32", [128, 32], "int32"), ("w1 w1c la lb lc", [128, 32], "float32"), ("lists", [128, 32], "uint16"),
+        ("onef bof bon edec", [128, 128], "float32"), ("sel", [128, 16, 128], "bfloat16"),
+        ("yci yc fbi sk sk2", [128, 8], "int32"), ("fb fs", [128, 8], "float32"),
+        ("jji q6 q8 kk0 kk1", [128, 4], "int32"), ("jj", [128, 4], "float32"),
+        ("km", [128, 64], "float32"), ("fmask fsp0 fsp1", [128, 1024], "bfloat16"),
+        ("eoi dui d6 ka pri", [128, 48], "int32"), ("ad", [128, 40], "int32"),
+        ("segm eoc dum c48 cf cc cs cl prf kr ctf cd so cpr cl2 bv eqv ss cod cle scb sc2 fv tot", [128, 48], "float32"),
+        ("jx0 jx1", [128, 8, 256], "bfloat16"), ("ms", [128, 256], "bfloat16"),
+        ("hx", [128, 2, 48], "int32"), ("sch", [128, 5, 128], "int32"),
+        ("eq", [128, 200], "float32"), ("m1", [128, 80], "float32"),
+        ("soff cdl", [128, 48], "uint16"), ("fl dec", [128, 8], "uint16"),
+        ("eall aa hit bb", [128, NDUM], "float32"), ("ypt", [128, 1024], "float32"),
+        ("l30 l31", [128, 2], "uint16"), ("lst0 lst1 lf0 lf1", [128, 4], "uint16"), ("eu0 eu1", [128, 64], "uint16"),
+        ("fr0 fr1", [128, 6 * 1024], "bfloat16"), ("dr0 dr1", [128, 768], "bfloat16"),
+        ("ab0 ab1", [128, 4, 256], "bfloat16"), ("rg0 rg1", [128, 256], "bfloat16")):
+    for _m in _n.split():
+        SCRATCH[_m] = ("sbuf", _s, _d)
+for _m in "kp0 kp1 pd0 pd1 pnew pmis".split():
+    SCRATCH[_m] = ("psum", [128, 512], "float32")
+SEMAPHORES = ("cv cs ct cg lpk0 lpk1 lrt ljc lsr lfx rw1 rw2 rf1 rf2 lsend oyf oyp0 oyp1 oyp2 oyp3").split()
+LNAMES = ("FWD", "FWD8", "REV", "ROUT", "PRR", "TRL", "TRS")
+LISTS = ((8, -47, 0, "q6"), (8, -47, -8, "q6"), (-1, 12, 5, "q6"), (-8, 49, 40, "q6"), (-8, 49, 32, "q6"),
+         (6, -47, 0, "q8"), (6, -49, 5, "q8"))
+
+
+def make_flow(g, T):
+    queues = {"v": g.vector, "s": g.scalar, "t": g.tensor, "g": g, "y": g.sync}
+    know = {q: {} for q in queues}
+    total, clocks, writer, readers = {}, {}, {}, {}
+
+    def need(q, toks):
+        worst = {}
+        for sem, val in toks:
+            if know[q].get(sem, 0) < val:
+                worst[sem] = max(worst.get(sem, 0), val)
+        for sem, val in sorted(worst.items()):
+            if know[q].get(sem, 0) < val:
+                queues[q].wait_ge(T.sem[sem], val)
+                for k, n in clocks[(sem, val)].items():
+                    know[q][k] = max(know[q].get(k, 0), n)
+
+    def deps(reads, writes):
+        toks = [writer[r] for r in reads if r in writer]
+        for w in writes:
+            if w in writer:
+                toks.append(writer[w])
+            toks += readers.get(w, [])
+        return toks
+
+    def stamp(q, name, inc):
+        total[name] = total.get(name, 0) + inc
+        clocks[(name, total[name])] = {**know[q], name: total[name]}
+
+    def done(tok, reads, writes):
+        for r in reads:
+            readers.setdefault(r, []).append(tok)
+        for w in writes:
+            writer[w] = tok
+            readers[w] = []
+
+    def op(q, calls, reads, writes, sem=None, inc=1):
+        need(q, deps(reads, writes))
+        name = sem or "c" + q
+        for c in (calls if isinstance(calls, list) else [calls]):
+            c(queues[q]).then_inc(T.sem[name], inc)
+            stamp(q, name, inc)
+        done((name, total[name]), reads, writes)
+
+    def send(call, reads, lsem, n):
+        need("g", deps(reads, []))
+        call(g)
+        stamp("g", lsem, n)
+        done((lsem, total[lsem]), reads, [])
+
+    def lands(name, sem, n):
+        total[sem] = n
+        clocks[(sem, n)] = {sem: n}
+        done((sem, n), [], [name])
+
+    def finish():
+        for sem, n in sorted(total.items()):
+            if know["g"].get(sem, 0) < n:
+                g.wait_ge(T.sem[sem], n)
+    return op, send, lands, finish
+
+
+def rank_program(g, core, T, topo):
+    rank = T.rank_of(core)
+    if rank is None:
+        return
+    N = len(T.cores)
+    op, send, lands, finish = make_flow(g, T)
+
+    def V(fn, r, w):
+        op("v", fn, r, w)
+
+    def G(fn, r, w):
+        op("g", fn, r, w)
+
+    def Sc(fn, r, w):
+        op("s", fn, r, w)
+
+    op("y", lambda e: e.dma_start(T.jci[:], T.jc[:]), [], ["jci"], "ljc", 16)
+    op("s", lambda e: e.dma_start(T.sri[:], T.sr[:]), [], ["sri"], "lsr", 16)
+    op("y", lambda e: e.dma_start(T.pkt[:, 0:512], T.pk[:, 0:512]), [], ["pkt0"], "lpk0", 16)
+    op("s", lambda e: e.dma_start(T.fin0[:], T.fx[:]), [], ["fin0"], "lfx", 16)
+    op("y", lambda e: e.dma_start(T.pkt[:, 512:1024], T.pk[:, 512:1024]), [], ["pkt1"], "lpk1", 16)
+    op("s", lambda e: e.dma_start(T.rtt[:], T.rt[:]), [], ["rtt"], "lrt", 16)
+    for t in (1, 2):
+        lands("fw%d" % t, "rw%d" % t, len(topo.engines(T.cores[(rank - t) % N], core)))
+        lands("fin%d" % t, "rf%d" % t, len(topo.engines(T.cores[(rank - 1) % N], core)))
+
+    flag = {"allow_small_or_imprecise_dtypes": True}
+    G(lambda e: e.iota(T.pi[:], [[1, 1]], 0, 1), [], ["pi"])
+    G(lambda e: e.iota(T.io32[:], [[1, 32]], 0, 0), [], ["io32"])
+    V(lambda e: e.memset(T.onef[:], 1.0), [], ["onef"])
+    V(lambda e: e.memset(T.oneb[:], 1.0), [], ["oneb"])
+    G(lambda e: e.affine_select(T.bon[:], T.onef[:], [[-16, 8], [0, 16]], A.is_ge, 0.0, 0, 1), ["onef"], ["bon"])
+    G(lambda e: e.affine_select(T.bof[:], T.bon[:], [[16, 8], [0, 16]], A.is_ge, 0.0, 15, -1), ["bon"], ["bof"])
+    G(lambda e: e.affine_select(T.bo8[:], T.oneb[0:8, :], [[1, 128]], A.is_ge, 0.0, 0, -16), ["oneb"], ["bo8"])
+    G(lambda e: e.affine_select(T.bo8[:], T.bo8[:], [[-1, 128]], A.is_ge, 0.0, 15, 16), ["bo8"], ["bo8"])
+    G(lambda e: e.affine_select(T.idb[:], T.oneb[:], [[-1, 128]], A.is_equal, 0.0, 0, 1), ["oneb"], ["idb"])
+    G(lambda e: e.iota(T.yci[:], [[0, 2], [256, 4]], 0, 0), [], ["yci"])
+    G(lambda e: e.iota(T.fsp0[:], [[0, 1024]], 0, 0, **flag), [], ["fsp0", "fsp0q"])
+    G(lambda e: e.iota(T.fsp1[:], [[0, 1024]], 0, 0, **flag), [], ["fsp1", "fsp1q"])
+    V(lambda e: e.memset(T.sel[:], 0.0), [], ["sel"])
+    V(lambda e: e.tensor_scalar(T.yli[:], T.pi[:], 15, None, A.bitwise_and), ["pi"], ["yli"])
+    V(lambda e: e.memset(T.fmask[:], 1.0), [], ["fmask"])
+    V(lambda e: e.tensor_copy(T.ylf[:], T.yli[:]), ["yli"], ["ylf"])
+    V(lambda e: e.tensor_scalar(T.q2k[:], T.yli[:], 2048.0, None, A.mult), ["yli"], ["q2k"])
+    V(lambda e: e.tensor_scalar(T.y16[:], T.yli[:], 16.0, None, A.mult), ["yli"], ["y16"])
+    V(lambda e: e.tensor_scalar(T.w1[:], T.io32[:], T.ylf[:, 0:1], None, A.is_equal), ["io32", "ylf"], ["w1"])
+    V(lambda e: e.memset(T.fmask[:, 0::16], 0.0), ["fmask"], ["fmask"])
+    V(lambda e: e.memset(T.tab[:, 2048:], 0.0), [], ["tab"])
+    V(lambda e: e.memset(T.km[:], 0.0), [], ["km"])
+    SELK = ["sel%d" % y for y in range(16)]
+    for y in range(16):
+        Sc(lambda e: e.activation(T.sel[:, y, y::16], T.bof[:, 0::16], AF.Copy, scale=32768.0), ["bof", "sel"], ["sel%d" % y])
+    V(lambda e: e.tensor_scalar(T.jh[:], T.jci[:], 8, None, A.arith_shift_right), ["jci"], ["jh"])
+    V(lambda e: e.tensor_scalar(T.jl[:], T.jci[:], 255, None, A.bitwise_and), ["jci"], ["jl"])
+    V(lambda e: e.memset(T.km[:, 0::16], 1.0e9), ["km"], ["km"])
+    V(lambda e: e.tensor_copy(T.jlb[:], T.jl[:]), ["jl"], ["jlb"])
+    V(lambda e: e.tensor_scalar(T.jhb[:], T.jh[:], 256.0, T.q2k[:, 0:1], A.mult, A.add), ["jh", "q2k"], ["jhb"])
+    V(lambda e: e.tensor_copy(T.srb[:], T.sri[:]), ["sri"], ["srb"])
+    op("t", lambda e: e.matmul(T.pnew[:, 0:128], T.bo8[:], T.srb[:], True, True), ["bo8", "srb"], ["pnew"])
+    for q in range(16):
+        V(lambda e: e.tensor_scalar(T.jx0[:, :, q::16], T.jhb[:], T.w1[:, q:q + 1], None, A.mult), ["jhb", "w1"], ["jx0_%d" % q])
+        Sc(lambda e: e.activation(T.jx1[:, :, q::16], T.jlb[:], AF.Copy, scale=T.w1[:, q:q + 1]), ["jlb", "w1"], ["jx1_%d" % q])
+    V(lambda e: e.tensor_scalar(T.oh[:], T.pnew[:, 0:128], T.ylf[:, 0:1], None, A.is_equal), ["pnew", "ylf"], ["oh"])
+    V(lambda e: e.tensor_scalar(T.yc[:], T.yci[:], T.y16[:, 0:1], None, A.add), ["yci", "y16"], ["yc"])
+    V(lambda e: e.tensor_tensor(T.ms[:, 0:128], T.oh[:], T.jhb[:], A.mult), ["oh", "jhb"], ["ms0"])
+    V(lambda e: e.tensor_tensor(T.ms[:, 128:256], T.oh[:], T.jlb[:], A.mult), ["oh", "jlb"], ["ms1"])
+    V(lambda e: e.tensor_scalar(T.idn[:], T.idb[:], -1.0, None, A.mult), ["idb"], ["idn"])
+    for lo in (0, 4):
+        V(lambda e: e.tensor_copy(T.yc[:, lo + 3:lo + 4], T.yc[:, lo:lo + 1]), ["yc"], ["yc"])
+    op("t", [lambda e, y=y: e.matmul(T.pd0[:, 256:272], T.sel[:, y, :], T.ms[:, y::16], y == 0, y == 15)
+             for y in range(16)], SELK + ["ms0", "ms1"], ["pd0"])
+    for i, b in enumerate(("jx0", "jx1")):
+        op("t", [lambda e, y=y: e.matmul(T.pd0[:, i * 128:(i + 1) * 128], T.sel[:, y, :], T[b][:, :, y * 16:y * 16 + 16], y == 0, y == 15)
+                 for y in range(16)], SELK + ["%s_%d" % (b, q) for q in range(16)], ["pd0"])
+    Sc(lambda e: e.activation(T.fw0[:], T.pd0[:, 0:272], AF.Copy, scale=1.0 / 32768.0), ["pd0"], ["fw0"])
+    for t in (1, 2):
+        dst = T.cores[(rank + t) % N]
+        rid, pid = topo.addr(dst, core)
+        send(lambda e: e.remote_dma(T["fw%d" % t][:], T.fw0[:], T.sem["rw%d" % t], T.sem.lsend, pid, rid, topo.mask(core, dst)),
+             ["fw0"], "lsend", len(topo.engines(core, dst)))
+    G(lambda e: e.iota(T.jji[:], [[16, 4]], 0, 0), [], ["jji"])
+    G(lambda e: e.iota(T.eoi[:], [[16, 8], [128, 6]], 0, 0), [], ["eoi"])
+    G(lambda e: e.iota(T.dui[:], [[16, 8], [-128, 6]], 2048 + 640, 0), [], ["dui"])
+    G(lambda e: e.iota(T.fbi[:], [[0, 2], [256, 4]], 5 * 1024, 0), [], ["fbi"])
+    for h in "01":
+        G(lambda e: e.iota(T["fr" + h][:, 5120:6144], [[0, 1024]], 0, 0, **flag), [], ["fr%s_5" % h, "fr%s_5q" % h])
+    TABK = ["tab"] + ["tab%d%d" % (i, j) for i in range(2) for j in range(2)]
+    for i in range(2):
+        a, b = 512 * i, 512 * i + 512
+        V(lambda e: e.tensor_scalar(T.tmpi[:, a:b], T.pkt[:, a:b], 4095, None, A.bitwise_and), ["pkt%d" % i], ["tmpi%d" % i])
+        V(lambda e: e.tensor_scalar(T.pkt[:, a:b], T.pkt[:, a:b], 12, None, A.arith_shift_right), ["pkt%d" % i], ["pkt%d" % i])
+        V(lambda e: e.tensor_copy(T.tab[:, a:b], T.tmpi[:, a:b]), ["tmpi%d" % i], ["tab%d0" % i])
+        V(lambda e: e.tensor_copy(T.tab[:, 1024 + a:1024 + b], T.pkt[:, a:b]), ["pkt%d" % i], ["tab%d1" % i])
+
+    def late_constants():
+        V(lambda e: e.memset(T.segm[:], 1.0), [], ["segm"])
+        V(lambda e: e.tensor_scalar(T.jj[:], T.jji[:], T.ylf[:, 0:1], None, A.add), ["jji", "ylf"], ["jj"])
+        for n in ("eq", "c48", "cl", "cd", "fv", "pri"):
+            V(lambda e: e.memset(T[n][:], 0), [], [n])
+        V(lambda e: e.tensor_scalar(T.q6[:], T.jj[:], 1.0 / 6.0, -2.5 / 6.0, A.mult, A.add), ["jj"], ["q6"])
+        V(lambda e: e.tensor_scalar(T.q8[:], T.jj[:], 0.125, -3.5 / 8.0, A.mult, A.add), ["jj"], ["q8"])
+        V(lambda e: e.memset(T.hx[:, 0, 40:48], 0), [], ["hx5"])
+        V(lambda e: e.memset(T.segm[:, 0::6], 0.0), ["segm"], ["segm"])
+        n = 4 * len(LISTS)
+        for i, (a, b, c, q) in enumerate(LISTS):
+            V(lambda e: e.tensor_scalar(T.la[:, 4 * i:4 * i + 4], T.jj[:], float(a), float(c), A.mult, A.add), ["jj"], ["la%d" % i])
+            V(lambda e: e.tensor_scalar(T.lb[:, 4 * i:4 * i + 4], T[q][:], float(b), None, A.mult), [q], ["lb%d" % i])
+        V(lambda e: e.tensor_tensor(T.lc[:, 0:n], T.la[:, 0:n], T.lb[:, 0:n], A.add),
+          [x % i for x in ("la%d", "lb%d") for i in range(len(LISTS))], ["lc"])
+        V(lambda e: e.tensor_scalar(T.eoc[:], T.eoi[:], T.ylf[:, 0:1], None, A.add), ["eoi", "ylf"], ["eoc"])
+        V(lambda e: e.tensor_copy(T.lists[:, 0:n], T.lc[:, 0:n]), ["lc"], ["lists"])
+        V(lambda e: e.tensor_scalar(T.dum[:], T.dui[:], T.ylf[:, 0:1], None, A.add), ["dui", "ylf"], ["dum"])
+        V(lambda e: e.tensor_scalar(T.w1c[:], T.w1[:], -1.0, 1.0, A.mult, A.add), ["w1"], ["w1c"])
+        V(lambda e: e.tensor_scalar(T.bon[:], T.bof[:], -1.0, None, A.mult), ["bof"], ["bon"])
+        V(lambda e: e.tensor_scalar(T.fb[:], T.fbi[:], T.y16[:, 0:1], 1.0 / 1024.0, A.add, A.mult), ["fbi", "y16"], ["fb"])
+
+    HXA = ["hxa0", "hxa1"]
+    HXB = ["hxb0", "hxb1"]
+
+    def start_keys(t):
+        fw = "fw%d" % t
+        V(lambda e: e.tensor_tensor(T.sk[:], T[fw][:, 256:264], T[fw][:, 264:272], A.add), [fw], ["sk"])
+        V(lambda e: e.tensor_scalar(T.hx[:, 0, 0:8], T.sk[:], 2047, None, A.bitwise_and), ["sk"], HXA)
+        V(lambda e: e.tensor_scalar(T.sk2[:], T.sk[:], 11, 15, A.arith_shift_right, A.bitwise_and), ["sk"], ["sk2"])
+        for h in "01":
+            lo = 4 * int(h)
+            V(lambda e: e.tensor_copy(T["lst" + h][:], T.hx[:, 0, lo:lo + 4]), ["hxa" + h], ["lst" + h])
+        V(lambda e: e.tensor_tensor(T.hx[:, 1, 0:8], T.sk2[:], T.yc[:], A.add), ["sk2", "yc"], HXB)
+
+    def start_facts(h, t):
+        fin = "fin%d" % t
+        lo = 64 * int(h)
+        Sc(lambda e: e.activation(T["fsp" + h][:, 0::16], T[fin][:, lo:lo + 64], AF.Copy), [fin], ["fsp" + h, "fsp" + h + "q"])
+
+    def entries(h):
+        V(lambda e: e.tensor_copy(T["eu" + h][:], T.tab[:].indirect(T["lst" + h][:])), TABK + ["lst" + h], ["eu" + h])
+
+    def spread(h, s):
+        V(lambda e: e.tensor_tensor_scan(T["fr" + h][:, 1024 * s:1024 * s + 1024], T.fmask[:], T["fsp" + h][:], 0.0, A.mult, A.add),
+          ["fmask", "fsp" + h, "fsp" + h + "q"], ["fr%s_%d" % (h, s)])
+
+    def post(h, s):
+        lo = 64 * int(h)
+        c = s * 8 + 4 * int(h)
+        key = T.sch[:, s - 1, lo + 15:lo + 64:16]
+        sch, lst, lf, l3 = "sch%d%s" % (s, h), "lst" + h, "lf" + h, "l3" + h
+        V(lambda e: e.tensor_tensor_scan(T.sch[:, s - 1, lo:lo + 64], T.km[:], T["kp" + h][:, 0:64], 0.0, A.max, A.min),
+          ["km", "kp" + h], [sch])
+        V(lambda e: e.tensor_scalar(T["kk" + h][:], key, 11, 15, A.arith_shift_right, A.bitwise_and), [sch], ["kk" + h])
+        if s < S:
+            V(lambda e: e.tensor_scalar(T.hx[:, 0, c:c + 4], key, 2047, None, A.bitwise_and), [sch], ["hxa" + h])
+        V(lambda e: e.tensor_tensor(T.hx[:, 1, c:c + 4], T["kk" + h][:], T.yc[:, 4 * int(h):4 * int(h) + 4], A.add),
+          ["kk" + h, "yc"], ["hxb" + h])
+        if s < S:
+            V(lambda e: e.tensor_copy(T[lst][:], T.hx[:, 0, c:c + 4]), ["hxa" + h], [lst])
+        V(lambda e: e.tensor_copy(T[lf][:], T.hx[:, 1, c:c + 4]), ["hxb" + h], [lf])
+        V(lambda e: e.tensor_copy(T[l3][:, 0:1], T.hx[:, 1, c + 3:c + 4]), ["hxb" + h], [l3])
+        if s < S:
+            dst, b, key = T["fsp" + h], 0, "fsp" + h
+        else:
+            dst, b, key = T["fr" + h], 5120, "fr%s_5" % h
+        Sc(lambda e: e.activation(dst[:, b:b + 768:16], T["dr" + h][:].indirect(T[lf][:, 0:3]), AF.Abs),
+           ["dr%sc0" % h, "dr%sc1" % h, lf], [key])
+        Sc(lambda e: e.activation(dst[:, b + 768:b + 1024:16], T["ab" + h][:, 3, :].indirect(T[l3][:, 0:1]), AF.Copy),
+           ["ab%s2" % h, l3], [key + "q"])
+        if s < S:
+            entries(h)
+
+    def gather(h, s, i):
+        eu, fr, dr = "eu" + h, "fr" + h, "dr" + h
+        a, b = ((0, 2), (2, 3))[i]
+        f0 = 1024 * (s - 1)
+        V(lambda e: e.tensor_tensor(T[dr][:, 256 * a:256 * b], T.rtt[:].indirect(T[eu][:, 16 * a:16 * b]),
+                                    T[fr][:, f0 + 256 * a:f0 + 256 * b], A.subtract),
+          ["rtt", eu, "fr%s_%d" % (h, s - 1)], [dr + "c%d" % i])
+
+    def begin(h, s, t):
+        eu, fr, dr, ab, rg, pd, kp = (n + h for n in ("eu", "fr", "dr", "ab", "rg", "pd", "kp"))
+        f0 = 1024 * (s - 1)
+        Sc(lambda e: e.activation(T[rg][:], T.rtt[:].indirect(T[eu][:, 48:64]), AF.Copy), ["rtt", eu], [rg])
+        gather(h, s, 0)
+        op("t", [lambda e: e.matmul(T[pd][:, 0:256], T.idb[:], T[rg][:], True, False),
+                 lambda e: e.matmul(T[pd][:, 0:256], T.idn[:], T[fr][:, f0 + 768:f0 + 1024], False, True)],
+           ["idb", "idn", rg, "fr%s_%d" % (h, s - 1)], [pd])
+        fw = "fw%d" % t
+        lo = 64 * int(h)
+        op("t", [lambda e: e.matmul(T[kp][:, 0:64], T.idb[:], T[fw][:, lo:lo + 64], True, False),
+                 lambda e: e.matmul(T[kp][:, 0:64], T.idb[:], T[fw][:, 128 + lo:128 + lo + 64], False, False)], ["idb", fw], [kp])
+        Sc(lambda e: e.activation(T[ab][:, 0:2, :], T[dr][:, 0:512], AF.Abs), [dr + "c0"], [ab + "0"])
+        Sc(lambda e: e.activation(T[ab][:, 3, :], T[pd][:, 0:256], AF.Abs), [pd], [ab + "2"])
+
+    def end(h, s):
+        dr, ab, kp = "dr" + h, "ab" + h, "kp" + h
+        gather(h, s, 1)
+        Sc(lambda e: e.activation(T[ab][:, 2, :], T[dr][:, 512:768], AF.Abs), [dr + "c1"], [ab + "1"])
+        op("t", [lambda e, y=y: e.matmul(T[kp][:, 0:64], T.sel[:, y, :], T[ab][:, :, y * 16:y * 16 + 16], False, y == 15)
+                 for y in range(16)], SELK + [ab + "0", ab + "1", ab + "2"], [kp])
+
+    def L(name):
+        i = LNAMES.index(name)
+        return T.lists[:, 4 * i:4 * i + 3]
+
+    def close(t):
+        EQK = ["eq"] + ["eq%d" % d for d in range(1, 6)]
+        for d in range(1, 6):
+            V(lambda e: e.tensor_tensor(T.eq[:, 48 * (d - 1):40 * d], T.hx[:, 1, 8 * d:48], T.hx[:, 1, 0:48 - 8 * d], A.is_equal),
+              HXB + ["eq"], ["eq%d" % d])
+        V(lambda e: e.tensor_scalar(T.prf[:], T.hx[:, 1, :].indirect(L("ROUT")), 1.0, None, A.add), HXB + ["lists"], ["prf"])
+        V(lambda e: e.tensor_tensor(T.m1[:], T.eq[:, 0:80], T.eq[:, 80:160], A.max), EQK, ["m1"])
+        V(lambda e: e.tensor_scalar(T.ka[:], T.hx[:, 1, :], 15, None, A.bitwise_and), HXB, ["ka"])
+        V(lambda e: e.tensor_tensor(T.m1[:, 0:40], T.m1[:, 0:40], T.m1[:, 40:80], A.max), ["m1"], ["m1"])
+        V(lambda e: e.tensor_copy(T.ctf[:], T.hx[:, 0, :].indirect(L("FWD8"))), HXA + ["hx5", "lists"], ["ctf"])
+        V(lambda e: e.tensor_tensor(T.c48[:, 8:48], T.m1[:, 0:40], T.eq[:, 160:200], A.max), ["m1", "c48"] + EQK, ["c48"])
+        V(lambda e: e.tensor_scalar(T.kr[:], T.ka[:].indirect(L("ROUT")), -31.0, None, A.add), ["ka", "lists"], ["kr"])
+        V(lambda e: e.tensor_copy(T.cf[:], T.c48[:].indirect(L("FWD"))), ["c48", "lists"], ["cf"])
+        V(lambda e: e.tensor_scalar(T.d6[:, 8:48], T.sch[:, :, 15::16], 15, None, A.arith_shift_right),
+          ["sch%d%s" % (s, h) for s in range(1, 6) for h in "01"], ["d6"])
+        V(lambda e: e.tensor_tensor_scan(T.cc[:], T.segm[:], T.cf[:], 0.0, A.mult, A.max), ["segm", "cf"], ["cc"])
+        V(lambda e: e.tensor_tensor(T.ad[:], T.d6[:, 8:48], T.d6[:, 0:40], A.add), ["d6", "d60"], ["ad"])
+        V(lambda e: e.tensor_tensor(T.cl[:, 1:48], T.cc[:, 1:48], T.cc[:, 0:47], A.is_gt), ["cc", "cl"], ["cl"])
+        V(lambda e: e.tensor_tensor(T.cd[:, 1:48], T.cc[:, 0:47], T.dum[:, 1:48], A.mult), ["cc", "dum", "cd"], ["cd"])
+        V(lambda e: e.tensor_tensor_scan(T.cs[:], T.segm[:], T.cc[:], 0.0, A.mult, A.add), ["segm", "cc"], ["cs"])
+        V(lambda e: e.tensor_tensor(T.cpr[:], T.cl[:].indirect(L("REV")), T.prf[:], A.mult), ["cl", "prf", "lists"], ["cpr"])
+        V(lambda e: e.tensor_tensor(T.so[:], T.cd[:], T.ctf[:], A.max), ["cd", "ctf"], ["so"])
+        V(lambda e: e.tensor_tensor(T.fs[:], T.fb[:], T.cs[:, 4::6], A.subtract), ["fb", "cs"], ["fs"])
+        V(lambda e: e.tensor_tensor_scan(T.bv[:], T.segm[:], T.cpr[:], 0.0, A.mult, A.add), ["segm", "cpr"], ["bv"])
+        V(lambda e: e.tensor_copy(T.soff[:], T.so[:].indirect(L("TRS"))), ["so", "lists"], ["soff"])
+        V(lambda e: e.tensor_scalar(T.fl[:], T.fs[:], 1024.0, None, A.mult), ["fs"], ["fl"])
+        for h in "01":
+            lo = 64 * int(h)
+            Sc(lambda e: e.activation(T.fout[:, lo:lo + 64], T["fr" + h][:].indirect(T.fl[:, 4 * int(h):4 * int(h) + 4]), AF.Copy),
+               ["fl"] + ["fr%s_%d" % (h, s) for s in range(6)] + ["fr%s_5q" % h], ["fout" + h])
+        if t < VI - 1:
+            dst = T.cores[(rank + 1) % N]
+            rid, pid = topo.addr(dst, core)
+            send(lambda e: e.remote_dma(T["fin%d" % (t + 1)][:], T.fout[:], T.sem["rf%d" % (t + 1)], T.sem.lsend, pid, rid,
+                                        topo.mask(core, dst)), ["fout0", "fout1"], "lsend", len(topo.engines(core, dst)))
+        else:
+            op("y", lambda e: e.dma_start(T.yf[:], T.fout[:]), ["fout0", "fout1"], ["yf"], "oyf", 16)
+        Sc(lambda e: e.activation(T.eall[:], T.tab[:].indirect(T.soff[:, 0:40]), AF.Copy), TABK + ["soff"], ["eall"])
+        V(lambda e: e.tensor_scalar(T.cl2[:], T.cl[:].indirect(L("REV")), 2.0, None, A.mult), ["cl", "lists"], ["cl2"])
+        V(lambda e: e.tensor_tensor(T.eqv[:], T.bv[:], T.prf[:], A.is_equal), ["bv", "prf"], ["eqv"])
+        V(lambda e: e.tensor_tensor(T.cle[:], T.cl[:].indirect(L("REV")), T.eoc[:], A.mult), ["cl", "eoc", "lists"], ["cle"])
+        V(lambda e: e.tensor_tensor_scan(T.ss[:], T.cl2[:], T.eqv[:], 0.0, A.add, A.subtract), ["cl2", "eqv"], ["ss"])
+        if t > 0:
+            V(lambda e: e.tensor_scalar(T.ad[:], T.ad[:], T.zc[:, 0:1], None, A.add), ["ad", "zc"], ["ad"])
+        V(lambda e: e.tensor_tensor(T.cod[:], T.ss[:], T.kr[:], A.mult), ["ss", "kr"], ["cod"])
+        V(lambda e: e.tensor_tensor_scan(T.scb[:], T.segm[:], T.cle[:], 0.0, A.mult, A.add), ["segm", "cle"], ["scb"])
+        V(lambda e: e.tensor_scalar(T.cdl[:], T.cod[:].indirect(L("TRL")), 31.0, None, A.add), ["cod", "lists"], ["cdl"])
+        Sc(lambda e: e.activation(T.hit[:], T.w1[:].indirect(T.cdl[:, 0:40]), AF.Copy), ["w1", "cdl"], ["hit"])
+        V(lambda e: e.tensor_scalar(T.pri[:, 0:40], T.ad[:], 1, None, A.bitwise_and), ["ad", "pri"], ["pri"])
+        V(lambda e: e.tensor_tensor(T.sc2[:], T.scb[:], T.eoc[:], A.subtract), ["scb", "eoc"], ["sc2"])
+        V(lambda e: e.tensor_tensor(T.fv[:, 0:47], T.ss[:, 0:47], T.ss[:, 1:48], A.is_gt), ["ss", "fv"], ["fv"])
+        V(lambda e: e.tensor_tensor(T.sc2[:], T.pri[:].indirect(L("PRR")), T.sc2[:], A.mult), ["pri", "sc2", "lists"], ["sc2"])
+        V(lambda e: e.tensor_tensor(T.sc2[:], T.sc2[:], T.eoc[:], A.add), ["sc2", "eoc"], ["sc2"])
+        V(lambda e: e.tensor_tensor(T.sc2[:], T.sc2[:], T.fv[:], A.mult), ["sc2", "fv"], ["sc2"])
+        V(lambda e: e.tensor_tensor_scan(T.tot[:], T.segm[:], T.sc2[:], 0.0, A.mult, A.add), ["segm", "sc2"], ["tot"])
+        V(lambda e: e.tensor_copy(T.dec[:], T.tot[:, 5::6]), ["tot"], ["dec"])
+        Sc(lambda e: e.activation(T.edec[:], T.eall[:].indirect(T.dec[:]), AF.Copy), ["eall", "dec"], ["edec"])
+        V(lambda e: e.tensor_tensor(T.aa[:], T.w1c[:].indirect(T.cdl[:, 0:40]), T.eall[:], A.mult), ["w1c", "cdl", "eall"], ["aa"])
+        V(lambda e: e.tensor_tensor(T.edec[:], T.aa[:].indirect(T.dec[:]), T.edec[:], A.subtract), ["aa", "dec", "edec"], ["edec"])
+        op("t", lambda e: e.matmul(T.pnew[:, 0:128], T.bon[:], T.edec[:], True, True), ["bon", "edec"], ["pnew"])
+        if t < VI - 1:
+            V(lambda e: e.tensor_reduce(T.zr[:], T.cc[:, 5::6], AxisListType.X, A.add), ["cc"], ["zr"])
+            op("t", lambda e: e.matmul(T.pmis[:, 0:1], T.onef[:], T.zr[:], True, True), ["onef", "zr"], ["pmis"])
+            start_keys(t + 1)
+        for r in range(5):
+            V(lambda e: e.tensor_tensor(T.bb[:, 128 * r:128 * r + 128], T.pnew[:, 0:128], T.hit[:, 128 * r:128 * r + 128], A.mult),
+              ["pnew", "hit"], ["bb%d" % r])
+        V(lambda e: e.tensor_tensor(T.tab[:].indirect(T.soff[:, 0:40]), T.aa[:], T.bb[:], A.add),
+          ["aa", "soff"] + TABK + ["bb%d" % r for r in range(5)], ["tab"])
+
+    start_keys(0)
+    for t in range(VI):
+        fin = "fin%d" % t
+        start_facts("0", t)
+        start_facts("1", t)
+        op("t", [lambda e, y=y: e.matmul(T.pmis[:, 8:16], T.sel[:, y, :], T[fin][:, y::16], y == 0, y == 15) for y in range(16)],
+           SELK + [fin], ["pmis"])
+        entries("0")
+        spread("0", 0)
+        begin("0", 1, t)
+        entries("1")
+        end("0", 1)
+        spread("1", 0)
+        begin("1", 1, t)
+        V(lambda e: e.tensor_scalar(T.d6[:, 0:8], T.pmis[:, 8:16], 1.0 / 32768.0, None, A.mult), ["pmis"], ["d60"])
+        if t == 1:
+            V(lambda e: e.tensor_copy(T.zc[:], T.pmis[:, 0:1]), ["pmis"], ["zc"])
+        elif t == 2:
+            V(lambda e: e.tensor_tensor(T.zc[:], T.pmis[:, 0:1], T.zc[:], A.add), ["pmis", "zc"], ["zc"])
+        if t == 0:
+            late_constants()
+        for s in range(1, S + 1):
+            post("0", s)
+            end("1", s)
+            if s < S:
+                spread("0", s)
+                begin("0", s + 1, t)
+            post("1", s)
+            if s < S:
+                end("0", s + 1)
+                spread("1", s)
+                begin("1", s + 1, t)
+        close(t)
+
+    for i in range(4):
+        pd, o = "pd%d" % (i % 2), 256 * i
+        Sc(lambda e: e.activation(T[pd][:, 0:256], T.tab[:, 1024 + o:1280 + o], AF.Copy, scale=4096.0), TABK, [pd])
+        V(lambda e: e.tensor_tensor(T.ypt[:, o:o + 256], T[pd][:, 0:256], T.tab[:, o:o + 256], A.add), [pd] + TABK, ["ypt%d" % i])
+        op("y", lambda e: e.dma_start(T.yp[:, o:o + 256], T.ypt[:, o:o + 256]), ["ypt%d" % i], ["yp%d" % i], "oyp%d" % i, 16)
+    finish()

@@ -12,17 +12,17 @@ for _n, _s, _d in (
         ("pi yli", [128, 1], "int32"), ("ylf y16 q2k zr zc", [128, 1], "float32"),
         ("io32", [128, 32], "int32"), ("w1 w1c la lb lc", [128, 32], "float32"), ("lists", [128, 32], "uint16"),
         ("onef bof bon edec", [128, 128], "float32"), ("sel", [128, 16, 128], "bfloat16"),
-        ("yci yc fbi sk sk2", [128, 8], "int32"), ("fb fs", [128, 8], "float32"),
-        ("jji q6 q8 kk0 kk1", [128, 4], "int32"), ("jj", [128, 4], "float32"),
+        ("sk", [128, 8], "int32"), ("fbi fb fs", [128, 8], "float32"),
+        ("jji q6 q8", [128, 4], "int32"), ("jj q6f q8f", [128, 4], "float32"),
         ("km", [128, 64], "float32"), ("fmask fsp0 fsp1", [128, 1024], "bfloat16"),
-        ("eoi dui d6 ka pri", [128, 48], "int32"), ("ad", [128, 40], "int32"),
-        ("segm eoc dum c48 cf cc cs cl prf kr ctf cd so cpr cl2 bv eqv ss cod cle scb sc2 fv tot", [128, 48], "float32"),
+        ("d6 pri", [128, 48], "int32"), ("ad", [128, 40], "int32"),
+        ("segm eoi dui eoc dum c48 cf cc cs cl prf kr ctf cd so cpr cl2 bv eqv ss cod cle scb sc2 fv tot", [128, 48], "float32"),
         ("jx0 jx1", [128, 8, 256], "bfloat16"), ("ms", [128, 256], "bfloat16"),
         ("hx", [128, 2, 48], "int32"), ("sch", [128, 5, 128], "int32"),
         ("eq", [128, 200], "float32"), ("m1", [128, 80], "float32"),
-        ("soff cdl", [128, 48], "uint16"), ("fl dec", [128, 8], "uint16"),
+        ("soff cdl", [128, 48], "uint16"), ("fl dec lf0 lf1", [128, 8], "uint16"),
         ("eall aa hit bb", [128, NDUM], "float32"), ("ypt", [128, 1024], "float32"),
-        ("l30 l31", [128, 2], "uint16"), ("lst0 lst1 lf0 lf1", [128, 4], "uint16"), ("eu0 eu1", [128, 64], "uint16"),
+        ("lst0 lst1", [128, 4], "uint16"), ("eu0 eu1", [128, 64], "uint16"),
         ("fr0 fr1", [128, 6 * 1024], "bfloat16"), ("dr0 dr1", [128, 768], "bfloat16"),
         ("ab0 ab1", [128, 4, 256], "bfloat16"), ("rg0 rg1", [128, 256], "bfloat16")):
     for _m in _n.split():
@@ -39,6 +39,7 @@ def make_flow(g, T):
     queues = {"v": g.vector, "s": g.scalar, "t": g.tensor, "g": g, "y": g.sync}
     know = {q: {} for q in queues}
     total, clocks, writer, readers = {}, {}, {}, {}
+    batch, collect = [], [False]
 
     def need(q, toks):
         worst = {}
@@ -59,10 +60,6 @@ def make_flow(g, T):
             toks += readers.get(w, [])
         return toks
 
-    def stamp(q, name, inc):
-        total[name] = total.get(name, 0) + inc
-        clocks[(name, total[name])] = {**know[q], name: total[name]}
-
     def done(tok, reads, writes):
         for r in reads:
             readers.setdefault(r, []).append(tok)
@@ -70,30 +67,71 @@ def make_flow(g, T):
             writer[w] = tok
             readers[w] = []
 
-    def op(q, calls, reads, writes, sem=None, inc=1):
+    def schedule():
+        lag = 0.12
+        w, rd, pred = {}, {}, []
+        for i, it in enumerate(batch):
+            p = {w[r] for r in it[2] if r in w}
+            for x in it[3]:
+                p |= ({w[x]} if x in w else set()) | rd.get(x, set())
+            for r in it[2]:
+                rd.setdefault(r, set()).add(i)
+            for x in it[3]:
+                w[x] = i
+                rd[x] = set()
+            pred.append(p - {i})
+        prio = [it[6] for it in batch]
+        for i in range(len(batch) - 1, -1, -1):
+            for p in pred[i]:
+                prio[p] = max(prio[p], batch[p][6] + lag + prio[i])
+        free, endt, left = {}, {}, list(range(len(batch)))
+        while left:
+            best = None
+            for i in left:
+                if all(p in endt for p in pred[i]):
+                    st = max([free.get(batch[i][0], 0.0)] + [endt[p] + lag for p in pred[i]])
+                    k = (round(st, 3), -prio[i], i)
+                    best = k if best is None or k < best else best
+            i = best[2]
+            left.remove(i)
+            endt[i] = best[0] + batch[i][6]
+            free[batch[i][0]] = endt[i]
+            issue(*batch[i][:6])
+        batch.clear()
+
+    def op(q, calls, reads, writes, sem=None, inc=1, dur=0.06):
+        if collect[0]:
+            batch.append((q, calls, reads, writes, sem, inc, dur))
+        else:
+            issue(q, calls, reads, writes, sem, inc)
+
+    def issue(q, calls, reads, writes, sem, inc):
+        remote = q == "r"
+        q = "g" if remote else q
         need(q, deps(reads, writes))
         name = sem or "c" + q
         for c in (calls if isinstance(calls, list) else [calls]):
-            c(queues[q]).then_inc(T.sem[name], inc)
-            stamp(q, name, inc)
+            if remote:
+                c(queues[q])
+            else:
+                c(queues[q]).then_inc(T.sem[name], inc)
+            total[name] = total.get(name, 0) + inc
+            clocks[(name, total[name])] = {**know[q], name: total[name]}
         done((name, total[name]), reads, writes)
 
     def send(call, reads, lsem, n):
-        need("g", deps(reads, []))
-        call(g)
-        stamp("g", lsem, n)
-        done((lsem, total[lsem]), reads, [])
+        op("r", call, reads, [], lsem, n, 1.0)
 
-    def lands(name, sem, n):
+    def lands(names, sem, n):
         total[sem] = n
         clocks[(sem, n)] = {sem: n}
-        done((sem, n), [], [name])
+        done((sem, n), [], list(names))
 
     def finish():
         for sem, n in sorted(total.items()):
             if know["g"].get(sem, 0) < n:
                 g.wait_ge(T.sem[sem], n)
-    return op, send, lands, finish
+    return op, send, lands, finish, collect, schedule
 
 
 def rank_program(g, core, T, topo):
@@ -101,16 +139,16 @@ def rank_program(g, core, T, topo):
     if rank is None:
         return
     N = len(T.cores)
-    op, send, lands, finish = make_flow(g, T)
+    op, send, lands, finish, collect, schedule = make_flow(g, T)
 
-    def V(fn, r, w):
-        op("v", fn, r, w)
+    def V(fn, r, w, dur=0.06):
+        op("v", fn, r, w, dur=dur)
 
     def G(fn, r, w):
         op("g", fn, r, w)
 
-    def Sc(fn, r, w):
-        op("s", fn, r, w)
+    def Sc(fn, r, w, dur=0.12):
+        op("s", fn, r, w, dur=dur)
 
     op("y", lambda e: e.dma_start(T.jci[:], T.jc[:]), [], ["jci"], "ljc", 16)
     op("s", lambda e: e.dma_start(T.sri[:], T.sr[:]), [], ["sri"], "lsr", 16)
@@ -119,8 +157,8 @@ def rank_program(g, core, T, topo):
     op("y", lambda e: e.dma_start(T.pkt[:, 512:1024], T.pk[:, 512:1024]), [], ["pkt1"], "lpk1", 16)
     op("s", lambda e: e.dma_start(T.rtt[:], T.rt[:]), [], ["rtt"], "lrt", 16)
     for t in (1, 2):
-        lands("fw%d" % t, "rw%d" % t, len(topo.engines(T.cores[(rank - t) % N], core)))
-        lands("fin%d" % t, "rf%d" % t, len(topo.engines(T.cores[(rank - 1) % N], core)))
+        lands(("fw%d" % t, "fws%d" % t), "rw%d" % t, len(topo.engines(T.cores[(rank - t) % N], core)))
+        lands(("fin%d" % t,), "rf%d" % t, len(topo.engines(T.cores[(rank - 1) % N], core)))
 
     flag = {"allow_small_or_imprecise_dtypes": True}
     G(lambda e: e.iota(T.pi[:], [[1, 1]], 0, 1), [], ["pi"])
@@ -132,9 +170,12 @@ def rank_program(g, core, T, topo):
     G(lambda e: e.affine_select(T.bo8[:], T.oneb[0:8, :], [[1, 128]], A.is_ge, 0.0, 0, -16), ["oneb"], ["bo8"])
     G(lambda e: e.affine_select(T.bo8[:], T.bo8[:], [[-1, 128]], A.is_ge, 0.0, 15, 16), ["bo8"], ["bo8"])
     G(lambda e: e.affine_select(T.idb[:], T.oneb[:], [[-1, 128]], A.is_equal, 0.0, 0, 1), ["oneb"], ["idb"])
-    G(lambda e: e.iota(T.yci[:], [[0, 2], [256, 4]], 0, 0), [], ["yci"])
-    G(lambda e: e.iota(T.fsp0[:], [[0, 1024]], 0, 0, **flag), [], ["fsp0", "fsp0q"])
-    G(lambda e: e.iota(T.fsp1[:], [[0, 1024]], 0, 0, **flag), [], ["fsp1", "fsp1q"])
+    G(lambda e: e.iota(T.jji[:], [[16, 4]], 0, 0), [], ["jji"])
+    G(lambda e: e.iota(T.eoi[:], [[16, 8], [128, 6]], 0, 0, **flag), [], ["eoi"])
+    G(lambda e: e.iota(T.dui[:], [[16, 8], [-128, 6]], 2048 + 640, 0, **flag), [], ["dui"])
+    G(lambda e: e.iota(T.fbi[:], [[0, 2], [256, 4]], 5 * 1024, 0, **flag), [], ["fbi"])
+    for h in "01":
+        G(lambda e: e.iota(T["fsp" + h][:], [[0, 1024]], 0, 0, **flag), [], ["fsp%s_%d" % (h, b) for b in range(4)])
     V(lambda e: e.memset(T.sel[:], 0.0), [], ["sel"])
     V(lambda e: e.tensor_scalar(T.yli[:], T.pi[:], 15, None, A.bitwise_and), ["pi"], ["yli"])
     V(lambda e: e.memset(T.fmask[:], 1.0), [], ["fmask"])
@@ -159,29 +200,38 @@ def rank_program(g, core, T, topo):
         V(lambda e: e.tensor_scalar(T.jx0[:, :, q::16], T.jhb[:], T.w1[:, q:q + 1], None, A.mult), ["jhb", "w1"], ["jx0_%d" % q])
         Sc(lambda e: e.activation(T.jx1[:, :, q::16], T.jlb[:], AF.Copy, scale=T.w1[:, q:q + 1]), ["jlb", "w1"], ["jx1_%d" % q])
     V(lambda e: e.tensor_scalar(T.oh[:], T.pnew[:, 0:128], T.ylf[:, 0:1], None, A.is_equal), ["pnew", "ylf"], ["oh"])
-    V(lambda e: e.tensor_scalar(T.yc[:], T.yci[:], T.y16[:, 0:1], None, A.add), ["yci", "y16"], ["yc"])
     V(lambda e: e.tensor_tensor(T.ms[:, 0:128], T.oh[:], T.jhb[:], A.mult), ["oh", "jhb"], ["ms0"])
     V(lambda e: e.tensor_tensor(T.ms[:, 128:256], T.oh[:], T.jlb[:], A.mult), ["oh", "jlb"], ["ms1"])
-    V(lambda e: e.tensor_scalar(T.idn[:], T.idb[:], -1.0, None, A.mult), ["idb"], ["idn"])
-    for lo in (0, 4):
-        V(lambda e: e.tensor_copy(T.yc[:, lo + 3:lo + 4], T.yc[:, lo:lo + 1]), ["yc"], ["yc"])
-    op("t", [lambda e, y=y: e.matmul(T.pd0[:, 256:272], T.sel[:, y, :], T.ms[:, y::16], y == 0, y == 15)
-             for y in range(16)], SELK + ["ms0", "ms1"], ["pd0"])
+    op("t", [lambda e, y=y: e.matmul(T.pd1[:, 0:16], T.sel[:, y, :], T.ms[:, y::16], y == 0, y == 15)
+             for y in range(16)], SELK + ["ms0", "ms1"], ["pd1"])
+    Sc(lambda e: e.activation(T.fw0[:, 256:272], T.pd1[:, 0:16], AF.Copy, scale=1.0 / 32768.0), ["pd1"], ["fws0"])
     for i, b in enumerate(("jx0", "jx1")):
         op("t", [lambda e, y=y: e.matmul(T.pd0[:, i * 128:(i + 1) * 128], T.sel[:, y, :], T[b][:, :, y * 16:y * 16 + 16], y == 0, y == 15)
                  for y in range(16)], SELK + ["%s_%d" % (b, q) for q in range(16)], ["pd0"])
-    Sc(lambda e: e.activation(T.fw0[:], T.pd0[:, 0:272], AF.Copy, scale=1.0 / 32768.0), ["pd0"], ["fw0"])
+    V(lambda e: e.memset(T.segm[:], 1.0), [], ["segm"])
+    V(lambda e: e.tensor_scalar(T.jj[:], T.jji[:], T.ylf[:, 0:1], None, A.add), ["jji", "ylf"], ["jj"])
+    V(lambda e: e.tensor_scalar(T.fb[:], T.fbi[:], T.y16[:, 0:1], 1.0 / 1024.0, A.add, A.mult), ["fbi", "y16"], ["fb"])
+    V(lambda e: e.tensor_scalar(T.q6[:], T.jj[:], 1.0 / 6.0, -2.5 / 6.0, A.mult, A.add), ["jj"], ["q6"])
+    V(lambda e: e.tensor_scalar(T.q8[:], T.jj[:], 0.125, -3.5 / 8.0, A.mult, A.add), ["jj"], ["q8"])
+    V(lambda e: e.memset(T.segm[:, 0::6], 0.0), ["segm"], ["segm"])
+    V(lambda e: e.tensor_copy(T.q6f[:], T.q6[:]), ["q6"], ["q6f"])
+    V(lambda e: e.tensor_copy(T.q8f[:], T.q8[:]), ["q8"], ["q8f"])
+    for i, (a, b, c, q) in enumerate(LISTS):
+        Sc(lambda e: e.activation(T.la[:, 4 * i:4 * i + 4], T.jj[:], AF.Copy, scale=float(a), bias=float(c)), ["jj"], ["la%d" % i])
+        Sc(lambda e: e.activation(T.lb[:, 4 * i:4 * i + 4], T[q + "f"][:], AF.Copy, scale=float(b)), [q + "f"], ["lb%d" % i])
+    Sc(lambda e: e.activation(T.fw0[:, 0:256], T.pd0[:, 0:256], AF.Copy, scale=1.0 / 32768.0), ["pd0"], ["fw0"])
+    Sc(lambda e: e.activation(T.idn[:], T.idb[:], AF.Copy, scale=-1.0), ["idb"], ["idn"])
     for t in (1, 2):
         dst = T.cores[(rank + t) % N]
         rid, pid = topo.addr(dst, core)
         send(lambda e: e.remote_dma(T["fw%d" % t][:], T.fw0[:], T.sem["rw%d" % t], T.sem.lsend, pid, rid, topo.mask(core, dst)),
-             ["fw0"], "lsend", len(topo.engines(core, dst)))
-    G(lambda e: e.iota(T.jji[:], [[16, 4]], 0, 0), [], ["jji"])
-    G(lambda e: e.iota(T.eoi[:], [[16, 8], [128, 6]], 0, 0), [], ["eoi"])
-    G(lambda e: e.iota(T.dui[:], [[16, 8], [-128, 6]], 2048 + 640, 0), [], ["dui"])
-    G(lambda e: e.iota(T.fbi[:], [[0, 2], [256, 4]], 5 * 1024, 0), [], ["fbi"])
+             ["fw0", "fws0"], "lsend", len(topo.engines(core, dst)))
+    for n in ("eq", "c48", "cl", "cd", "fv"):
+        G(lambda e: e.iota(T[n][:], [[0, T[n].shape[1]]], 0, 0, **flag), [], [n])
+    G(lambda e: e.iota(T.pri[:], [[0, 48]], 0, 0), [], ["pri"])
+    G(lambda e: e.iota(T.hx[:, 0, 40:48], [[0, 8]], 0, 0), [], ["hx5"])
     for h in "01":
-        G(lambda e: e.iota(T["fr" + h][:, 5120:6144], [[0, 1024]], 0, 0, **flag), [], ["fr%s_5" % h, "fr%s_5q" % h])
+        G(lambda e: e.iota(T["fr" + h][:, 5120:6144], [[0, 1024]], 0, 0, **flag), [], ["fr%s_5_%d" % (h, b) for b in range(4)])
     TABK = ["tab"] + ["tab%d%d" % (i, j) for i in range(2) for j in range(2)]
     for i in range(2):
         a, b = 512 * i, 512 * i + 512
@@ -190,109 +240,82 @@ def rank_program(g, core, T, topo):
         V(lambda e: e.tensor_copy(T.tab[:, a:b], T.tmpi[:, a:b]), ["tmpi%d" % i], ["tab%d0" % i])
         V(lambda e: e.tensor_copy(T.tab[:, 1024 + a:1024 + b], T.pkt[:, a:b]), ["pkt%d" % i], ["tab%d1" % i])
 
-    def late_constants():
-        V(lambda e: e.memset(T.segm[:], 1.0), [], ["segm"])
-        V(lambda e: e.tensor_scalar(T.jj[:], T.jji[:], T.ylf[:, 0:1], None, A.add), ["jji", "ylf"], ["jj"])
-        for n in ("eq", "c48", "cl", "cd", "fv", "pri"):
-            V(lambda e: e.memset(T[n][:], 0), [], [n])
-        V(lambda e: e.tensor_scalar(T.q6[:], T.jj[:], 1.0 / 6.0, -2.5 / 6.0, A.mult, A.add), ["jj"], ["q6"])
-        V(lambda e: e.tensor_scalar(T.q8[:], T.jj[:], 0.125, -3.5 / 8.0, A.mult, A.add), ["jj"], ["q8"])
-        V(lambda e: e.memset(T.hx[:, 0, 40:48], 0), [], ["hx5"])
-        V(lambda e: e.memset(T.segm[:, 0::6], 0.0), ["segm"], ["segm"])
-        n = 4 * len(LISTS)
-        for i, (a, b, c, q) in enumerate(LISTS):
-            V(lambda e: e.tensor_scalar(T.la[:, 4 * i:4 * i + 4], T.jj[:], float(a), float(c), A.mult, A.add), ["jj"], ["la%d" % i])
-            V(lambda e: e.tensor_scalar(T.lb[:, 4 * i:4 * i + 4], T[q][:], float(b), None, A.mult), [q], ["lb%d" % i])
-        V(lambda e: e.tensor_tensor(T.lc[:, 0:n], T.la[:, 0:n], T.lb[:, 0:n], A.add),
-          [x % i for x in ("la%d", "lb%d") for i in range(len(LISTS))], ["lc"])
-        V(lambda e: e.tensor_scalar(T.eoc[:], T.eoi[:], T.ylf[:, 0:1], None, A.add), ["eoi", "ylf"], ["eoc"])
-        V(lambda e: e.tensor_copy(T.lists[:, 0:n], T.lc[:, 0:n]), ["lc"], ["lists"])
-        V(lambda e: e.tensor_scalar(T.dum[:], T.dui[:], T.ylf[:, 0:1], None, A.add), ["dui", "ylf"], ["dum"])
-        V(lambda e: e.tensor_scalar(T.w1c[:], T.w1[:], -1.0, 1.0, A.mult, A.add), ["w1"], ["w1c"])
-        V(lambda e: e.tensor_scalar(T.bon[:], T.bof[:], -1.0, None, A.mult), ["bof"], ["bon"])
-        V(lambda e: e.tensor_scalar(T.fb[:], T.fbi[:], T.y16[:, 0:1], 1.0 / 1024.0, A.add, A.mult), ["fbi", "y16"], ["fb"])
-
     HXA = ["hxa0", "hxa1"]
     HXB = ["hxb0", "hxb1"]
 
     def start_keys(t):
         fw = "fw%d" % t
-        V(lambda e: e.tensor_tensor(T.sk[:], T[fw][:, 256:264], T[fw][:, 264:272], A.add), [fw], ["sk"])
+        V(lambda e: e.tensor_tensor(T.sk[:], T[fw][:, 256:264], T[fw][:, 264:272], A.add), ["fws%d" % t], ["sk"])
         V(lambda e: e.tensor_scalar(T.hx[:, 0, 0:8], T.sk[:], 2047, None, A.bitwise_and), ["sk"], HXA)
-        V(lambda e: e.tensor_scalar(T.sk2[:], T.sk[:], 11, 15, A.arith_shift_right, A.bitwise_and), ["sk"], ["sk2"])
+        V(lambda e: e.tensor_scalar(T.hx[:, 1, 0:8], T.sk[:], 11, 15, A.arith_shift_right, A.bitwise_and), ["sk"], HXB)
         for h in "01":
             lo = 4 * int(h)
-            V(lambda e: e.tensor_copy(T["lst" + h][:], T.hx[:, 0, lo:lo + 4]), ["hxa" + h], ["lst" + h])
-        V(lambda e: e.tensor_tensor(T.hx[:, 1, 0:8], T.sk2[:], T.yc[:], A.add), ["sk2", "yc"], HXB)
+            V(lambda e, h=h, lo=lo: e.tensor_copy(T["lst" + h][:], T.hx[:, 0, lo:lo + 4]), ["hxa" + h], ["lst" + h])
 
     def start_facts(h, t):
         fin = "fin%d" % t
         lo = 64 * int(h)
-        Sc(lambda e: e.activation(T["fsp" + h][:, 0::16], T[fin][:, lo:lo + 64], AF.Copy), [fin], ["fsp" + h, "fsp" + h + "q"])
+        Sc(lambda e: e.activation(T["fsp" + h][:, 0::16], T[fin][:, lo:lo + 64], AF.Copy), [fin], ["fsp%s_%d" % (h, b) for b in range(4)])
 
     def entries(h):
         V(lambda e: e.tensor_copy(T["eu" + h][:], T.tab[:].indirect(T["lst" + h][:])), TABK + ["lst" + h], ["eu" + h])
 
     def spread(h, s):
-        V(lambda e: e.tensor_tensor_scan(T["fr" + h][:, 1024 * s:1024 * s + 1024], T.fmask[:], T["fsp" + h][:], 0.0, A.mult, A.add),
-          ["fmask", "fsp" + h, "fsp" + h + "q"], ["fr%s_%d" % (h, s)])
+        for x, a, b in (("a", 0, 256), ("b", 256, 1024)):
+            V(lambda e: e.tensor_tensor_scan(T["fr" + h][:, 1024 * s + a:1024 * s + b], T.fmask[:, a:b], T["fsp" + h][:, a:b], 0.0, A.mult, A.add),
+              ["fmask"] + ["fsp%s_%d" % (h, i) for i in range(4)], ["fr%s_%d%s" % (h, s, x)])
 
     def post(h, s):
         lo = 64 * int(h)
         c = s * 8 + 4 * int(h)
         key = T.sch[:, s - 1, lo + 15:lo + 64:16]
-        sch, lst, lf, l3 = "sch%d%s" % (s, h), "lst" + h, "lf" + h, "l3" + h
+        sch, lst, lf = "sch%d%s" % (s, h), "lst" + h, "lf" + h
         V(lambda e: e.tensor_tensor_scan(T.sch[:, s - 1, lo:lo + 64], T.km[:], T["kp" + h][:, 0:64], 0.0, A.max, A.min),
           ["km", "kp" + h], [sch])
-        V(lambda e: e.tensor_scalar(T["kk" + h][:], key, 11, 15, A.arith_shift_right, A.bitwise_and), [sch], ["kk" + h])
+        V(lambda e: e.tensor_scalar(T.hx[:, 1, c:c + 4], key, 11, 15, A.arith_shift_right, A.bitwise_and), [sch], ["hxb" + h])
         if s < S:
             V(lambda e: e.tensor_scalar(T.hx[:, 0, c:c + 4], key, 2047, None, A.bitwise_and), [sch], ["hxa" + h])
-        V(lambda e: e.tensor_tensor(T.hx[:, 1, c:c + 4], T["kk" + h][:], T.yc[:, 4 * int(h):4 * int(h) + 4], A.add),
-          ["kk" + h, "yc"], ["hxb" + h])
+        V(lambda e: e.tensor_scalar(T[lf][:, 0::2], T.hx[:, 1, c:c + 4], T.y16[:, 0:1], None, A.add), ["hxb" + h, "y16"], [lf])
         if s < S:
             V(lambda e: e.tensor_copy(T[lst][:], T.hx[:, 0, c:c + 4]), ["hxa" + h], [lst])
-        V(lambda e: e.tensor_copy(T[lf][:], T.hx[:, 1, c:c + 4]), ["hxb" + h], [lf])
-        V(lambda e: e.tensor_copy(T[l3][:, 0:1], T.hx[:, 1, c + 3:c + 4]), ["hxb" + h], [l3])
-        if s < S:
-            dst, b, key = T["fsp" + h], 0, "fsp" + h
+            dst, o, fk = T["fsp" + h], 0, "fsp%s_" % h
         else:
-            dst, b, key = T["fr" + h], 5120, "fr%s_5" % h
-        Sc(lambda e: e.activation(dst[:, b:b + 768:16], T["dr" + h][:].indirect(T[lf][:, 0:3]), AF.Abs),
-           ["dr%sc0" % h, "dr%sc1" % h, lf], [key])
-        Sc(lambda e: e.activation(dst[:, b + 768:b + 1024:16], T["ab" + h][:, 3, :].indirect(T[l3][:, 0:1]), AF.Copy),
-           ["ab%s2" % h, l3], [key + "q"])
-        if s < S:
-            entries(h)
+            dst, o, fk = T["fr" + h], 5120, "fr%s_5_" % h
+        for b in range(4):
+            win = T["dr" + h][:, 256 * b:256 * b + 256] if b < 3 else T["ab" + h][:, 3, :]
+            Sc(lambda e, b=b, win=win: e.activation(dst[:, o + 256 * b:o + 256 * b + 256:16], win.indirect(T[lf][:, 2 * b:2 * b + 1]), AF.Abs),
+               [("dr%sc0", "dr%sc1", "dr%sc2", "ab%s3")[b] % h, lf], [fk + str(b)])
 
     def gather(h, s, i):
         eu, fr, dr = "eu" + h, "fr" + h, "dr" + h
-        a, b = ((0, 2), (2, 3))[i]
         f0 = 1024 * (s - 1)
-        V(lambda e: e.tensor_tensor(T[dr][:, 256 * a:256 * b], T.rtt[:].indirect(T[eu][:, 16 * a:16 * b]),
-                                    T[fr][:, f0 + 256 * a:f0 + 256 * b], A.subtract),
-          ["rtt", eu, "fr%s_%d" % (h, s - 1)], [dr + "c%d" % i])
+        V(lambda e: e.tensor_tensor(T[dr][:, 256 * i:256 * i + 256], T.rtt[:].indirect(T[eu][:, 16 * i:16 * i + 16]),
+                                    T[fr][:, f0 + 256 * i:f0 + 256 * i + 256], A.subtract),
+          ["rtt", eu, "fr%s_%d%s" % (h, s - 1, "abb"[i])], [dr + "c%d" % i], 0.37)
 
     def begin(h, s, t):
         eu, fr, dr, ab, rg, pd, kp = (n + h for n in ("eu", "fr", "dr", "ab", "rg", "pd", "kp"))
         f0 = 1024 * (s - 1)
         Sc(lambda e: e.activation(T[rg][:], T.rtt[:].indirect(T[eu][:, 48:64]), AF.Copy), ["rtt", eu], [rg])
         gather(h, s, 0)
+        gather(h, s, 1)
         op("t", [lambda e: e.matmul(T[pd][:, 0:256], T.idb[:], T[rg][:], True, False),
                  lambda e: e.matmul(T[pd][:, 0:256], T.idn[:], T[fr][:, f0 + 768:f0 + 1024], False, True)],
-           ["idb", "idn", rg, "fr%s_%d" % (h, s - 1)], [pd])
+           ["idb", "idn", rg, "fr%s_%db" % (h, s - 1)], [pd])
         fw = "fw%d" % t
         lo = 64 * int(h)
         op("t", [lambda e: e.matmul(T[kp][:, 0:64], T.idb[:], T[fw][:, lo:lo + 64], True, False),
                  lambda e: e.matmul(T[kp][:, 0:64], T.idb[:], T[fw][:, 128 + lo:128 + lo + 64], False, False)], ["idb", fw], [kp])
-        Sc(lambda e: e.activation(T[ab][:, 0:2, :], T[dr][:, 0:512], AF.Abs), [dr + "c0"], [ab + "0"])
-        Sc(lambda e: e.activation(T[ab][:, 3, :], T[pd][:, 0:256], AF.Abs), [pd], [ab + "2"])
+        for b in (0, 1):
+            Sc(lambda e, b=b: e.activation(T[ab][:, b, :], T[dr][:, 256 * b:256 * b + 256], AF.Abs), [dr + "c%d" % b], [ab + str(b)], 0.3)
 
     def end(h, s):
-        dr, ab, kp = "dr" + h, "ab" + h, "kp" + h
-        gather(h, s, 1)
-        Sc(lambda e: e.activation(T[ab][:, 2, :], T[dr][:, 512:768], AF.Abs), [dr + "c1"], [ab + "1"])
+        dr, ab, kp, pd = "dr" + h, "ab" + h, "kp" + h, "pd" + h
+        gather(h, s, 2)
+        Sc(lambda e: e.activation(T[ab][:, 3, :], T[pd][:, 0:256], AF.Abs), [pd], [ab + "3"], 0.3)
+        Sc(lambda e: e.activation(T[ab][:, 2, :], T[dr][:, 512:768], AF.Abs), [dr + "c2"], [ab + "2"], 0.3)
         op("t", [lambda e, y=y: e.matmul(T[kp][:, 0:64], T.sel[:, y, :], T[ab][:, :, y * 16:y * 16 + 16], False, y == 15)
-                 for y in range(16)], SELK + [ab + "0", ab + "1", ab + "2"], [kp])
+                 for y in range(16)], SELK + [ab + "0", ab + "1", ab + "2", ab + "3"], [kp], dur=0.75)
 
     def L(name):
         i = LNAMES.index(name)
@@ -301,16 +324,15 @@ def rank_program(g, core, T, topo):
     def close(t):
         EQK = ["eq"] + ["eq%d" % d for d in range(1, 6)]
         for d in range(1, 6):
-            V(lambda e: e.tensor_tensor(T.eq[:, 48 * (d - 1):40 * d], T.hx[:, 1, 8 * d:48], T.hx[:, 1, 0:48 - 8 * d], A.is_equal),
+            V(lambda e, d=d: e.tensor_tensor(T.eq[:, 48 * (d - 1):40 * d], T.hx[:, 1, 8 * d:48], T.hx[:, 1, 0:48 - 8 * d], A.is_equal),
               HXB + ["eq"], ["eq%d" % d])
-        V(lambda e: e.tensor_scalar(T.prf[:], T.hx[:, 1, :].indirect(L("ROUT")), 1.0, None, A.add), HXB + ["lists"], ["prf"])
+        V(lambda e: e.tensor_scalar(T.prf[:], T.hx[:, 1, :].indirect(L("ROUT")), 1.0, None, A.add), HXB + ["lists"], ["prf"], 0.11)
         V(lambda e: e.tensor_tensor(T.m1[:], T.eq[:, 0:80], T.eq[:, 80:160], A.max), EQK, ["m1"])
-        V(lambda e: e.tensor_scalar(T.ka[:], T.hx[:, 1, :], 15, None, A.bitwise_and), HXB, ["ka"])
         V(lambda e: e.tensor_tensor(T.m1[:, 0:40], T.m1[:, 0:40], T.m1[:, 40:80], A.max), ["m1"], ["m1"])
-        V(lambda e: e.tensor_copy(T.ctf[:], T.hx[:, 0, :].indirect(L("FWD8"))), HXA + ["hx5", "lists"], ["ctf"])
+        V(lambda e: e.tensor_copy(T.ctf[:], T.hx[:, 0, :].indirect(L("FWD8"))), HXA + ["hx5", "lists"], ["ctf"], 0.11)
         V(lambda e: e.tensor_tensor(T.c48[:, 8:48], T.m1[:, 0:40], T.eq[:, 160:200], A.max), ["m1", "c48"] + EQK, ["c48"])
-        V(lambda e: e.tensor_scalar(T.kr[:], T.ka[:].indirect(L("ROUT")), -31.0, None, A.add), ["ka", "lists"], ["kr"])
-        V(lambda e: e.tensor_copy(T.cf[:], T.c48[:].indirect(L("FWD"))), ["c48", "lists"], ["cf"])
+        V(lambda e: e.tensor_scalar(T.kr[:], T.hx[:, 1, :].indirect(L("ROUT")), -31.0, None, A.add), HXB + ["lists"], ["kr"], 0.11)
+        V(lambda e: e.tensor_copy(T.cf[:], T.c48[:].indirect(L("FWD"))), ["c48", "lists"], ["cf"], 0.11)
         V(lambda e: e.tensor_scalar(T.d6[:, 8:48], T.sch[:, :, 15::16], 15, None, A.arith_shift_right),
           ["sch%d%s" % (s, h) for s in range(1, 6) for h in "01"], ["d6"])
         V(lambda e: e.tensor_tensor_scan(T.cc[:], T.segm[:], T.cf[:], 0.0, A.mult, A.max), ["segm", "cf"], ["cc"])
@@ -318,16 +340,16 @@ def rank_program(g, core, T, topo):
         V(lambda e: e.tensor_tensor(T.cl[:, 1:48], T.cc[:, 1:48], T.cc[:, 0:47], A.is_gt), ["cc", "cl"], ["cl"])
         V(lambda e: e.tensor_tensor(T.cd[:, 1:48], T.cc[:, 0:47], T.dum[:, 1:48], A.mult), ["cc", "dum", "cd"], ["cd"])
         V(lambda e: e.tensor_tensor_scan(T.cs[:], T.segm[:], T.cc[:], 0.0, A.mult, A.add), ["segm", "cc"], ["cs"])
-        V(lambda e: e.tensor_tensor(T.cpr[:], T.cl[:].indirect(L("REV")), T.prf[:], A.mult), ["cl", "prf", "lists"], ["cpr"])
+        V(lambda e: e.tensor_tensor(T.cpr[:], T.cl[:].indirect(L("REV")), T.prf[:], A.mult), ["cl", "prf", "lists"], ["cpr"], 0.11)
         V(lambda e: e.tensor_tensor(T.so[:], T.cd[:], T.ctf[:], A.max), ["cd", "ctf"], ["so"])
         V(lambda e: e.tensor_tensor(T.fs[:], T.fb[:], T.cs[:, 4::6], A.subtract), ["fb", "cs"], ["fs"])
         V(lambda e: e.tensor_tensor_scan(T.bv[:], T.segm[:], T.cpr[:], 0.0, A.mult, A.add), ["segm", "cpr"], ["bv"])
-        V(lambda e: e.tensor_copy(T.soff[:], T.so[:].indirect(L("TRS"))), ["so", "lists"], ["soff"])
+        V(lambda e: e.tensor_copy(T.soff[:], T.so[:].indirect(L("TRS"))), ["so", "lists"], ["soff"], 0.11)
         V(lambda e: e.tensor_scalar(T.fl[:], T.fs[:], 1024.0, None, A.mult), ["fs"], ["fl"])
         for h in "01":
             lo = 64 * int(h)
-            Sc(lambda e: e.activation(T.fout[:, lo:lo + 64], T["fr" + h][:].indirect(T.fl[:, 4 * int(h):4 * int(h) + 4]), AF.Copy),
-               ["fl"] + ["fr%s_%d" % (h, s) for s in range(6)] + ["fr%s_5q" % h], ["fout" + h])
+            Sc(lambda e, h=h, lo=lo: e.activation(T.fout[:, lo:lo + 64], T["fr" + h][:].indirect(T.fl[:, 4 * int(h):4 * int(h) + 4]), AF.Copy),
+               ["fl"] + ["fr%s_%d%s" % (h, s, x) for s in range(5) for x in "ab"] + ["fr%s_5_%d" % (h, b) for b in range(4)], ["fout" + h])
         if t < VI - 1:
             dst = T.cores[(rank + 1) % N]
             rid, pid = topo.addr(dst, core)
@@ -335,38 +357,38 @@ def rank_program(g, core, T, topo):
                                         topo.mask(core, dst)), ["fout0", "fout1"], "lsend", len(topo.engines(core, dst)))
         else:
             op("y", lambda e: e.dma_start(T.yf[:], T.fout[:]), ["fout0", "fout1"], ["yf"], "oyf", 16)
-        Sc(lambda e: e.activation(T.eall[:], T.tab[:].indirect(T.soff[:, 0:40]), AF.Copy), TABK + ["soff"], ["eall"])
-        V(lambda e: e.tensor_scalar(T.cl2[:], T.cl[:].indirect(L("REV")), 2.0, None, A.mult), ["cl", "lists"], ["cl2"])
+        Sc(lambda e: e.activation(T.eall[:], T.tab[:].indirect(T.soff[:, 0:40]), AF.Copy), TABK + ["soff"], ["eall"], dur=0.86)
+        V(lambda e: e.tensor_scalar(T.cl2[:], T.cl[:].indirect(L("REV")), 2.0, None, A.mult), ["cl", "lists"], ["cl2"], 0.11)
         V(lambda e: e.tensor_tensor(T.eqv[:], T.bv[:], T.prf[:], A.is_equal), ["bv", "prf"], ["eqv"])
-        V(lambda e: e.tensor_tensor(T.cle[:], T.cl[:].indirect(L("REV")), T.eoc[:], A.mult), ["cl", "eoc", "lists"], ["cle"])
+        V(lambda e: e.tensor_tensor(T.cle[:], T.cl[:].indirect(L("REV")), T.eoc[:], A.mult), ["cl", "eoc", "lists"], ["cle"], 0.11)
         V(lambda e: e.tensor_tensor_scan(T.ss[:], T.cl2[:], T.eqv[:], 0.0, A.add, A.subtract), ["cl2", "eqv"], ["ss"])
         if t > 0:
             V(lambda e: e.tensor_scalar(T.ad[:], T.ad[:], T.zc[:, 0:1], None, A.add), ["ad", "zc"], ["ad"])
         V(lambda e: e.tensor_tensor(T.cod[:], T.ss[:], T.kr[:], A.mult), ["ss", "kr"], ["cod"])
         V(lambda e: e.tensor_tensor_scan(T.scb[:], T.segm[:], T.cle[:], 0.0, A.mult, A.add), ["segm", "cle"], ["scb"])
-        V(lambda e: e.tensor_scalar(T.cdl[:], T.cod[:].indirect(L("TRL")), 31.0, None, A.add), ["cod", "lists"], ["cdl"])
-        Sc(lambda e: e.activation(T.hit[:], T.w1[:].indirect(T.cdl[:, 0:40]), AF.Copy), ["w1", "cdl"], ["hit"])
+        V(lambda e: e.tensor_scalar(T.cdl[:], T.cod[:].indirect(L("TRL")), 31.0, None, A.add), ["cod", "lists"], ["cdl"], 0.11)
+        Sc(lambda e: e.activation(T.hit[:], T.w1[:].indirect(T.cdl[:, 0:40]), AF.Copy), ["w1", "cdl"], ["hit"], dur=0.86)
         V(lambda e: e.tensor_scalar(T.pri[:, 0:40], T.ad[:], 1, None, A.bitwise_and), ["ad", "pri"], ["pri"])
         V(lambda e: e.tensor_tensor(T.sc2[:], T.scb[:], T.eoc[:], A.subtract), ["scb", "eoc"], ["sc2"])
         V(lambda e: e.tensor_tensor(T.fv[:, 0:47], T.ss[:, 0:47], T.ss[:, 1:48], A.is_gt), ["ss", "fv"], ["fv"])
-        V(lambda e: e.tensor_tensor(T.sc2[:], T.pri[:].indirect(L("PRR")), T.sc2[:], A.mult), ["pri", "sc2", "lists"], ["sc2"])
+        V(lambda e: e.tensor_tensor(T.sc2[:], T.pri[:].indirect(L("PRR")), T.sc2[:], A.mult), ["pri", "sc2", "lists"], ["sc2"], 0.11)
         V(lambda e: e.tensor_tensor(T.sc2[:], T.sc2[:], T.eoc[:], A.add), ["sc2", "eoc"], ["sc2"])
         V(lambda e: e.tensor_tensor(T.sc2[:], T.sc2[:], T.fv[:], A.mult), ["sc2", "fv"], ["sc2"])
         V(lambda e: e.tensor_tensor_scan(T.tot[:], T.segm[:], T.sc2[:], 0.0, A.mult, A.add), ["segm", "sc2"], ["tot"])
         V(lambda e: e.tensor_copy(T.dec[:], T.tot[:, 5::6]), ["tot"], ["dec"])
-        Sc(lambda e: e.activation(T.edec[:], T.eall[:].indirect(T.dec[:]), AF.Copy), ["eall", "dec"], ["edec"])
-        V(lambda e: e.tensor_tensor(T.aa[:], T.w1c[:].indirect(T.cdl[:, 0:40]), T.eall[:], A.mult), ["w1c", "cdl", "eall"], ["aa"])
-        V(lambda e: e.tensor_tensor(T.edec[:], T.aa[:].indirect(T.dec[:]), T.edec[:], A.subtract), ["aa", "dec", "edec"], ["edec"])
-        op("t", lambda e: e.matmul(T.pnew[:, 0:128], T.bon[:], T.edec[:], True, True), ["bon", "edec"], ["pnew"])
+        Sc(lambda e: e.activation(T.edec[:], T.eall[:].indirect(T.dec[:]), AF.Copy), ["eall", "dec"], ["edec"], dur=0.22)
+        V(lambda e: e.tensor_tensor(T.aa[:], T.w1c[:].indirect(T.cdl[:, 0:40]), T.eall[:], A.mult), ["w1c", "cdl", "eall"], ["aa"], dur=0.85)
+        V(lambda e: e.tensor_tensor(T.edec[:], T.aa[:].indirect(T.dec[:]), T.edec[:], A.subtract), ["aa", "dec", "edec"], ["edec"], dur=0.21)
+        op("t", lambda e: e.matmul(T.pnew[:, 0:128], T.bon[:], T.edec[:], True, True), ["bon", "edec"], ["pnew"], dur=0.4)
         if t < VI - 1:
             V(lambda e: e.tensor_reduce(T.zr[:], T.cc[:, 5::6], AxisListType.X, A.add), ["cc"], ["zr"])
             op("t", lambda e: e.matmul(T.pmis[:, 0:1], T.onef[:], T.zr[:], True, True), ["onef", "zr"], ["pmis"])
             start_keys(t + 1)
         for r in range(5):
-            V(lambda e: e.tensor_tensor(T.bb[:, 128 * r:128 * r + 128], T.pnew[:, 0:128], T.hit[:, 128 * r:128 * r + 128], A.mult),
-              ["pnew", "hit"], ["bb%d" % r])
+            V(lambda e, r=r: e.tensor_tensor(T.bb[:, 128 * r:128 * r + 128], T.pnew[:, 0:128], T.hit[:, 128 * r:128 * r + 128], A.mult),
+              ["pnew", "hit"], ["bb%d" % r], dur=0.11)
         V(lambda e: e.tensor_tensor(T.tab[:].indirect(T.soff[:, 0:40]), T.aa[:], T.bb[:], A.add),
-          ["aa", "soff"] + TABK + ["bb%d" % r for r in range(5)], ["tab"])
+          ["aa", "soff"] + TABK + ["bb%d" % r for r in range(5)], ["tab"], dur=2.0)
 
     start_keys(0)
     for t in range(VI):
@@ -375,8 +397,8 @@ def rank_program(g, core, T, topo):
         start_facts("1", t)
         op("t", [lambda e, y=y: e.matmul(T.pmis[:, 8:16], T.sel[:, y, :], T[fin][:, y::16], y == 0, y == 15) for y in range(16)],
            SELK + [fin], ["pmis"])
-        entries("0")
         spread("0", 0)
+        entries("0")
         begin("0", 1, t)
         entries("1")
         end("0", 1)
@@ -388,19 +410,31 @@ def rank_program(g, core, T, topo):
         elif t == 2:
             V(lambda e: e.tensor_tensor(T.zc[:], T.pmis[:, 0:1], T.zc[:], A.add), ["pmis", "zc"], ["zc"])
         if t == 0:
-            late_constants()
+            n = 4 * len(LISTS)
+            V(lambda e: e.tensor_tensor(T.lc[:, 0:n], T.la[:, 0:n], T.lb[:, 0:n], A.add),
+              [x % i for x in ("la%d", "lb%d") for i in range(len(LISTS))], ["lc"])
+            Sc(lambda e: e.activation(T.eoc[:], T.eoi[:], AF.Identity, bias=T.ylf[:, 0:1]), ["eoi", "ylf"], ["eoc"])
+            Sc(lambda e: e.activation(T.dum[:], T.dui[:], AF.Identity, bias=T.ylf[:, 0:1]), ["dui", "ylf"], ["dum"])
+            Sc(lambda e: e.activation(T.w1c[:], T.w1[:], AF.Copy, scale=-1.0, bias=1.0), ["w1"], ["w1c"])
+            Sc(lambda e: e.activation(T.bon[:], T.bof[:], AF.Copy, scale=-1.0), ["bof"], ["bon"])
+            V(lambda e: e.tensor_copy(T.lists[:, 0:n], T.lc[:, 0:n]), ["lc"], ["lists"])
         for s in range(1, S + 1):
+            collect[0] = s == S
             post("0", s)
             end("1", s)
             if s < S:
+                entries("0")
                 spread("0", s)
                 begin("0", s + 1, t)
             post("1", s)
             if s < S:
                 end("0", s + 1)
+                entries("1")
                 spread("1", s)
                 begin("1", s + 1, t)
         close(t)
+        collect[0] = False
+        schedule()
 
     for i in range(4):
         pd, o = "pd%d" % (i % 2), 256 * i

from concourse.mybir import AluOpType, AxisListType, ActivationFunctionType

A = AluOpType
AF = ActivationFunctionType
VI, S = 3, 5
NDUM = 640
SCRATCH = {}
for _n, _s, _d in (
        ("pkt tmpi", [128, 1024], "int32"), ("rtt", [128, 3072], "bfloat16"), ("tab", [128, 2048 + NDUM], "float32"),
        ("jci jh jl", [128, 128], "int32"), ("sri", [8, 128], "int32"), ("srb bo8", [8, 128], "bfloat16"),
        ("fin0 fin1 fin2 fout oneb idb idn jhb jlb oh", [128, 128], "bfloat16"), ("fw0 fw1 fw2", [128, 272], "bfloat16"),
        ("pi yli", [128, 1], "int32"), ("ylf y16 q2k zr zc", [128, 1], "float32"),
        ("io32", [128, 32], "int32"), ("w1 w1c la lb lc", [128, 32], "float32"), ("lists", [128, 32], "uint16"),
        ("onef bof bon edec", [128, 128], "float32"), ("sel", [128, 16, 128], "bfloat16"),
        ("sk", [128, 8], "int32"), ("fbi fb fs", [128, 8], "float32"),
        ("jji q6 q8", [128, 4], "int32"), ("jj q6f q8f", [128, 4], "float32"),
        ("km", [128, 64], "float32"), ("fmask fsp0 fsp1", [128, 1024], "bfloat16"),
        ("d6 pri", [128, 48], "int32"), ("ad", [128, 40], "int32"),
        ("segm eoi dui eoc dum c48 cf cc cs cl prf kr ctf cd so cpr cl2 bv eqv ss cod cle scb sc2 fv tot", [128, 48], "float32"),
        ("jx0 jx1", [128, 8, 256], "bfloat16"), ("ms", [128, 256], "bfloat16"),
        ("hx", [128, 2, 48], "int32"), ("sch", [128, 5, 128], "int32"),
        ("eq", [128, 200], "float32"), ("m1", [128, 80], "float32"),
        ("soff cdl", [128, 48], "uint16"), ("fl dec lf0 lf1", [128, 8], "uint16"),
        ("eall aa hit bb", [128, NDUM], "float32"), ("ypt", [128, 1024], "float32"),
        ("lst0 lst1", [128, 4], "uint16"), ("eu0 eu1", [128, 64], "uint16"),
        ("fr0 fr1", [128, 6 * 1024], "bfloat16"), ("dr0 dr1", [128, 768], "bfloat16"),
        ("ab0 ab1", [128, 4, 256], "bfloat16"), ("rg0 rg1", [128, 256], "bfloat16")):
    for _m in _n.split():
        SCRATCH[_m] = ("sbuf", _s, _d)
for _m in "kp0 kp1 pd0 pd1 pnew pmis".split():
    SCRATCH[_m] = ("psum", [128, 512], "float32")
SEMAPHORES = ("cv cs ct cg lpk0 lpk1 lrt ljc lsr lfx rw1 rw2 rf1 rf2 lsend oyf oyp0 oyp1 oyp2 oyp3").split()
LNAMES = ("FWD", "FWD8", "REV", "ROUT", "PRR", "TRL", "TRS")
LISTS = ((8, -47, 0, "q6"), (8, -47, -8, "q6"), (-1, 12, 5, "q6"), (-8, 49, 40, "q6"), (-8, 49, 32, "q6"),
         (6, -47, 0, "q8"), (6, -49, 5, "q8"))


def make_flow(g, T):
    queues = {"v": g.vector, "s": g.scalar, "t": g.tensor, "g": g, "y": g.sync}
    know = {q: {} for q in queues}
    total, clocks, writer, readers = {}, {}, {}, {}
    batch, collect = [], [False]

    def need(q, toks):
        worst = {}
        for sem, val in toks:
            if know[q].get(sem, 0) < val:
                worst[sem] = max(worst.get(sem, 0), val)
        for sem, val in sorted(worst.items()):
            if know[q].get(sem, 0) < val:
                queues[q].wait_ge(T.sem[sem], val)
                for k, n in clocks[(sem, val)].items():
                    know[q][k] = max(know[q].get(k, 0), n)

    def deps(reads, writes):
        toks = [writer[r] for r in reads if r in writer]
        for w in writes:
            if w in writer:
                toks.append(writer[w])
            toks += readers.get(w, [])
        return toks

    def done(tok, reads, writes):
        for r in reads:
            readers.setdefault(r, []).append(tok)
        for w in writes:
            writer[w] = tok
            readers[w] = []

    def schedule():
        lag = 0.12
        w, rd, pred = {}, {}, []
        for i, it in enumerate(batch):
            p = {w[r] for r in it[2] if r in w}
            for x in it[3]:
                p |= ({w[x]} if x in w else set()) | rd.get(x, set())
            for r in it[2]:
                rd.setdefault(r, set()).add(i)
            for x in it[3]:
                w[x] = i
                rd[x] = set()
            pred.append(p - {i})
        prio = [it[6] for it in batch]
        for i in range(len(batch) - 1, -1, -1):
            for p in pred[i]:
                prio[p] = max(prio[p], batch[p][6] + lag + prio[i])
        free, endt, left = {}, {}, list(range(len(batch)))
        while left:
            best = None
            for i in left:
                if all(p in endt for p in pred[i]):
                    st = max([free.get(batch[i][0], 0.0)] + [endt[p] + lag for p in pred[i]])
                    k = (round(st, 3), -prio[i], i)
                    best = k if best is None or k < best else best
            i = best[2]
            left.remove(i)
            endt[i] = best[0] + batch[i][6]
            free[batch[i][0]] = endt[i]
            issue(*batch[i][:6])
        batch.clear()

    def op(q, calls, reads, writes, sem=None, inc=1, dur=0.06):
        if collect[0]:
            batch.append((q, calls, reads, writes, sem, inc, dur))
        else:
            issue(q, calls, reads, writes, sem, inc)

    def issue(q, calls, reads, writes, sem, inc):
        remote = q == "r"
        q = "g" if remote else q
        need(q, deps(reads, writes))
        name = sem or "c" + q
        for c in (calls if isinstance(calls, list) else [calls]):
            if remote:
                c(queues[q])
            else:
                c(queues[q]).then_inc(T.sem[name], inc)
            total[name] = total.get(name, 0) + inc
            clocks[(name, total[name])] = {**know[q], name: total[name]}
        done((name, total[name]), reads, writes)

    def send(call, reads, lsem, n):
        op("r", call, reads, [], lsem, n, 1.0)

    def lands(names, sem, n):
        total[sem] = n
        clocks[(sem, n)] = {sem: n}
        done((sem, n), [], list(names))

    def finish():
        for sem, n in sorted(total.items()):
            if know["g"].get(sem, 0) < n:
                g.wait_ge(T.sem[sem], n)
    return op, send, lands, finish, collect, schedule


def rank_program(g, core, T, topo):
    rank = T.rank_of(core)
    if rank is None:
        return
    N = len(T.cores)
    op, send, lands, finish, collect, schedule = make_flow(g, T)

    def V(fn, r, w, dur=0.06):
        op("v", fn, r, w, dur=dur)

    def G(fn, r, w):
        op("g", fn, r, w)

    def Sc(fn, r, w, dur=0.12):
        op("s", fn, r, w, dur=dur)

    op("y", lambda e: e.dma_start(T.jci[:], T.jc[:]), [], ["jci"], "ljc", 16)
    op("s", lambda e: e.dma_start(T.sri[:], T.sr[:]), [], ["sri"], "lsr", 16)
    op("y", lambda e: e.dma_start(T.pkt[:, 0:512], T.pk[:, 0:512]), [], ["pkt0"], "lpk0", 16)
    op("s", lambda e: e.dma_start(T.fin0[:], T.fx[:]), [], ["fin0"], "lfx", 16)
    op("y", lambda e: e.dma_start(T.pkt[:, 512:1024], T.pk[:, 512:1024]), [], ["pkt1"], "lpk1", 16)
    op("s", lambda e: e.dma_start(T.rtt[:], T.rt[:]), [], ["rtt"], "lrt", 16)
    for t in (1, 2):
        lands(("fw%d" % t, "fws%d" % t), "rw%d" % t, len(topo.engines(T.cores[(rank - t) % N], core)))
        lands(("fin%d" % t,), "rf%d" % t, len(topo.engines(T.cores[(rank - 1) % N], core)))

    flag = {"allow_small_or_imprecise_dtypes": True}
    G(lambda e: e.iota(T.pi[:], [[1, 1]], 0, 1), [], ["pi"])
    G(lambda e: e.iota(T.io32[:], [[1, 32]], 0, 0), [], ["io32"])
    V(lambda e: e.memset(T.onef[:], 1.0), [], ["onef"])
    V(lambda e: e.memset(T.oneb[:], 1.0), [], ["oneb"])
    G(lambda e: e.affine_select(T.bon[:], T.onef[:], [[-16, 8], [0, 16]], A.is_ge, 0.0, 0, 1), ["onef"], ["bon"])
    G(lambda e: e.affine_select(T.bof[:], T.bon[:], [[16, 8], [0, 16]], A.is_ge, 0.0, 15, -1), ["bon"], ["bof"])
    G(lambda e: e.affine_select(T.bo8[:], T.oneb[0:8, :], [[1, 128]], A.is_ge, 0.0, 0, -16), ["oneb"], ["bo8"])
    G(lambda e: e.affine_select(T.bo8[:], T.bo8[:], [[-1, 128]], A.is_ge, 0.0, 15, 16), ["bo8"], ["bo8"])
    G(lambda e: e.affine_select(T.idb[:], T.oneb[:], [[-1, 128]], A.is_equal, 0.0, 0, 1), ["oneb"], ["idb"])
    G(lambda e: e.iota(T.jji[:], [[16, 4]], 0, 0), [], ["jji"])
    G(lambda e: e.iota(T.eoi[:], [[16, 8], [128, 6]], 0, 0, **flag), [], ["eoi"])
    G(lambda e: e.iota(T.dui[:], [[16, 8], [-128, 6]], 2048 + 640, 0, **flag), [], ["dui"])
    G(lambda e: e.iota(T.fbi[:], [[0, 2], [256, 4]], 5 * 1024, 0, **flag), [], ["fbi"])
    for h in "01":
        G(lambda e: e.iota(T["fsp" + h][:], [[0, 1024]], 0, 0, **flag), [], ["fsp%s_%d" % (h, b) for b in range(4)])
    V(lambda e: e.memset(T.sel[:], 0.0), [], ["sel"])
    V(lambda e: e.tensor_scalar(T.yli[:], T.pi[:], 15, None, A.bitwise_and), ["pi"], ["yli"])
    V(lambda e: e.memset(T.fmask[:], 1.0), [], ["fmask"])
    V(lambda e: e.tensor_copy(T.ylf[:], T.yli[:]), ["yli"], ["ylf"])
    V(lambda e: e.tensor_scalar(T.q2k[:], T.yli[:], 2048.0, None, A.mult), ["yli"], ["q2k"])
    V(lambda e: e.tensor_scalar(T.y16[:], T.yli[:], 16.0, None, A.mult), ["yli"], ["y16"])
    V(lambda e: e.tensor_scalar(T.w1[:], T.io32[:], T.ylf[:, 0:1], None, A.is_equal), ["io32", "ylf"], ["w1"])
    V(lambda e: e.memset(T.fmask[:, 0::16], 0.0), ["fmask"], ["fmask"])
    V(lambda e: e.memset(T.tab[:, 2048:], 0.0), [], ["tab"])
    V(lambda e: e.memset(T.km[:], 0.0), [], ["km"])
    SELK = ["sel%d" % y for y in range(16)]
    for y in range(16):
        Sc(lambda e: e.activation(T.sel[:, y, y::16], T.bof[:, 0::16], AF.Copy, scale=32768.0), ["bof", "sel"], ["sel%d" % y])
    V(lambda e: e.tensor_scalar(T.jh[:], T.jci[:], 8, None, A.arith_shift_right), ["jci"], ["jh"])
    V(lambda e: e.tensor_scalar(T.jl[:], T.jci[:], 255, None, A.bitwise_and), ["jci"], ["jl"])
    V(lambda e: e.memset(T.km[:, 0::16], 1.0e9), ["km"], ["km"])
    V(lambda e: e.tensor_copy(T.jlb[:], T.jl[:]), ["jl"], ["jlb"])
    V(lambda e: e.tensor_scalar(T.jhb[:], T.jh[:], 256.0, T.q2k[:, 0:1], A.mult, A.add), ["jh", "q2k"], ["jhb"])
    V(lambda e: e.tensor_copy(T.srb[:], T.sri[:]), ["sri"], ["srb"])
    op("t", lambda e: e.matmul(T.pnew[:, 0:128], T.bo8[:], T.srb[:], True, True), ["bo8", "srb"], ["pnew"])
    for q in range(16):
        V(lambda e: e.tensor_scalar(T.jx0[:, :, q::16], T.jhb[:], T.w1[:, q:q + 1], None, A.mult), ["jhb", "w1"], ["jx0_%d" % q])
        Sc(lambda e: e.activation(T.jx1[:, :, q::16], T.jlb[:], AF.Copy, scale=T.w1[:, q:q + 1]), ["jlb", "w1"], ["jx1_%d" % q])
    V(lambda e: e.tensor_scalar(T.oh[:], T.pnew[:, 0:128], T.ylf[:, 0:1], None, A.is_equal), ["pnew", "ylf"], ["oh"])
    V(lambda e: e.tensor_tensor(T.ms[:, 0:128], T.oh[:], T.jhb[:], A.mult), ["oh", "jhb"], ["ms0"])
    V(lambda e: e.tensor_tensor(T.ms[:, 128:256], T.oh[:], T.jlb[:], A.mult), ["oh", "jlb"], ["ms1"])
    op("t", [lambda e, y=y: e.matmul(T.pd1[:, 0:16], T.sel[:, y, :], T.ms[:, y::16], y == 0, y == 15)
             for y in range(16)], SELK + ["ms0", "ms1"], ["pd1"])
    Sc(lambda e: e.activation(T.fw0[:, 256:272], T.pd1[:, 0:16], AF.Copy, scale=1.0 / 32768.0), ["pd1"], ["fws0"])
    for i, b in enumerate(("jx0", "jx1")):
        op("t", [lambda e, y=y: e.matmul(T.pd0[:, i * 128:(i + 1) * 128], T.sel[:, y, :], T[b][:, :, y * 16:y * 16 + 16], y == 0, y == 15)
                 for y in range(16)], SELK + ["%s_%d" % (b, q) for q in range(16)], ["pd0"])
    V(lambda e: e.memset(T.segm[:], 1.0), [], ["segm"])
    V(lambda e: e.tensor_scalar(T.jj[:], T.jji[:], T.ylf[:, 0:1], None, A.add), ["jji", "ylf"], ["jj"])
    V(lambda e: e.tensor_scalar(T.fb[:], T.fbi[:], T.y16[:, 0:1], 1.0 / 1024.0, A.add, A.mult), ["fbi", "y16"], ["fb"])
    V(lambda e: e.tensor_scalar(T.q6[:], T.jj[:], 1.0 / 6.0, -2.5 / 6.0, A.mult, A.add), ["jj"], ["q6"])
    V(lambda e: e.tensor_scalar(T.q8[:], T.jj[:], 0.125, -3.5 / 8.0, A.mult, A.add), ["jj"], ["q8"])
    V(lambda e: e.memset(T.segm[:, 0::6], 0.0), ["segm"], ["segm"])
    V(lambda e: e.tensor_copy(T.q6f[:], T.q6[:]), ["q6"], ["q6f"])
    V(lambda e: e.tensor_copy(T.q8f[:], T.q8[:]), ["q8"], ["q8f"])
    for i, (a, b, c, q) in enumerate(LISTS):
        Sc(lambda e: e.activation(T.la[:, 4 * i:4 * i + 4], T.jj[:], AF.Copy, scale=float(a), bias=float(c)), ["jj"], ["la%d" % i])
        Sc(lambda e: e.activation(T.lb[:, 4 * i:4 * i + 4], T[q + "f"][:], AF.Copy, scale=float(b)), [q + "f"], ["lb%d" % i])
    Sc(lambda e: e.activation(T.fw0[:, 0:256], T.pd0[:, 0:256], AF.Copy, scale=1.0 / 32768.0), ["pd0"], ["fw0"])
    Sc(lambda e: e.activation(T.idn[:], T.idb[:], AF.Copy, scale=-1.0), ["idb"], ["idn"])
    for t in (1, 2):
        dst = T.cores[(rank + t) % N]
        rid, pid = topo.addr(dst, core)
        send(lambda e: e.remote_dma(T["fw%d" % t][:], T.fw0[:], T.sem["rw%d" % t], T.sem.lsend, pid, rid, topo.mask(core, dst)),
             ["fw0", "fws0"], "lsend", len(topo.engines(core, dst)))
    for n in ("eq", "c48", "cl", "cd", "fv"):
        G(lambda e: e.iota(T[n][:], [[0, T[n].shape[1]]], 0, 0, **flag), [], [n])
    G(lambda e: e.iota(T.pri[:], [[0, 48]], 0, 0), [], ["pri"])
    G(lambda e: e.iota(T.hx[:, 0, 40:48], [[0, 8]], 0, 0), [], ["hx5"])
    for h in "01":
        G(lambda e: e.iota(T["fr" + h][:, 5120:6144], [[0, 1024]], 0, 0, **flag), [], ["fr%s_5_%d" % (h, b) for b in range(4)])
    TABK = ["tab"] + ["tab%d%d" % (i, j) for i in range(2) for j in range(2)]
    for i in range(2):
        a, b = 512 * i, 512 * i + 512
        V(lambda e: e.tensor_scalar(T.tmpi[:, a:b], T.pkt[:, a:b], 4095, None, A.bitwise_and), ["pkt%d" % i], ["tmpi%d" % i])
        V(lambda e: e.tensor_scalar(T.pkt[:, a:b], T.pkt[:, a:b], 12, None, A.arith_shift_right), ["pkt%d" % i], ["pkt%d" % i])
        V(lambda e: e.tensor_copy(T.tab[:, a:b], T.tmpi[:, a:b]), ["tmpi%d" % i], ["tab%d0" % i])
        V(lambda e: e.tensor_copy(T.tab[:, 1024 + a:1024 + b], T.pkt[:, a:b]), ["pkt%d" % i], ["tab%d1" % i])

    HXA = ["hxa0", "hxa1"]
    HXB = ["hxb0", "hxb1"]

    def start_keys(t):
        fw = "fw%d" % t
        V(lambda e: e.tensor_tensor(T.sk[:], T[fw][:, 256:264], T[fw][:, 264:272], A.add), ["fws%d" % t], ["sk"])
        V(lambda e: e.tensor_scalar(T.hx[:, 0, 0:8], T.sk[:], 2047, None, A.bitwise_and), ["sk"], HXA)
        V(lambda e: e.tensor_scalar(T.hx[:, 1, 0:8], T.sk[:], 11, 15, A.arith_shift_right, A.bitwise_and), ["sk"], HXB)
        for h in "01":
            lo = 4 * int(h)
            V(lambda e, h=h, lo=lo: e.tensor_copy(T["lst" + h][:], T.hx[:, 0, lo:lo + 4]), ["hxa" + h], ["lst" + h])

    def start_facts(h, t):
        fin = "fin%d" % t
        lo = 64 * int(h)
        Sc(lambda e: e.activation(T["fsp" + h][:, 0::16], T[fin][:, lo:lo + 64], AF.Copy), [fin], ["fsp%s_%d" % (h, b) for b in range(4)])

    def entries(h):
        V(lambda e: e.tensor_copy(T["eu" + h][:], T.tab[:].indirect(T["lst" + h][:])), TABK + ["lst" + h], ["eu" + h])

    def spread(h, s):
        for x, a, b in (("a", 0, 256), ("b", 256, 1024)):
            V(lambda e: e.tensor_tensor_scan(T["fr" + h][:, 1024 * s + a:1024 * s + b], T.fmask[:, a:b], T["fsp" + h][:, a:b], 0.0, A.mult, A.add),
              ["fmask"] + ["fsp%s_%d" % (h, i) for i in range(4)], ["fr%s_%d%s" % (h, s, x)])

    def post(h, s):
        lo = 64 * int(h)
        c = s * 8 + 4 * int(h)
        key = T.sch[:, s - 1, lo + 15:lo + 64:16]
        sch, lst, lf = "sch%d%s" % (s, h), "lst" + h, "lf" + h
        V(lambda e: e.tensor_tensor_scan(T.sch[:, s - 1, lo:lo + 64], T.km[:], T["kp" + h][:, 0:64], 0.0, A.max, A.min),
          ["km", "kp" + h], [sch])
        V(lambda e: e.tensor_scalar(T.hx[:, 1, c:c + 4], key, 11, 15, A.arith_shift_right, A.bitwise_and), [sch], ["hxb" + h])
        if s < S:
            V(lambda e: e.tensor_scalar(T.hx[:, 0, c:c + 4], key, 2047, None, A.bitwise_and), [sch], ["hxa" + h])
        V(lambda e: e.tensor_scalar(T[lf][:, 0::2], T.hx[:, 1, c:c + 4], T.y16[:, 0:1], None, A.add), ["hxb" + h, "y16"], [lf])
        if s < S:
            V(lambda e: e.tensor_copy(T[lst][:], T.hx[:, 0, c:c + 4]), ["hxa" + h], [lst])
            dst, o, fk = T["fsp" + h], 0, "fsp%s_" % h
        else:
            dst, o, fk = T["fr" + h], 5120, "fr%s_5_" % h
        for b in range(4):
            win = T["dr" + h][:, 256 * b:256 * b + 256] if b < 3 else T["ab" + h][:, 3, :]
            Sc(lambda e, b=b, win=win: e.activation(dst[:, o + 256 * b:o + 256 * b + 256:16], win.indirect(T[lf][:, 2 * b:2 * b + 1]), AF.Abs),
               [("dr%sc0", "dr%sc1", "dr%sc2", "ab%s3")[b] % h, lf], [fk + str(b)])

    def gather(h, s, i):
        eu, fr, dr = "eu" + h, "fr" + h, "dr" + h
        f0 = 1024 * (s - 1)
        V(lambda e: e.tensor_tensor(T[dr][:, 256 * i:256 * i + 256], T.rtt[:].indirect(T[eu][:, 16 * i:16 * i + 16]),
                                    T[fr][:, f0 + 256 * i:f0 + 256 * i + 256], A.subtract),
          ["rtt", eu, "fr%s_%d%s" % (h, s - 1, "abb"[i])], [dr + "c%d" % i], 0.37)

    def begin(h, s, t):
        eu, fr, dr, ab, rg, pd, kp = (n + h for n in ("eu", "fr", "dr", "ab", "rg", "pd", "kp"))
        f0 = 1024 * (s - 1)
        Sc(lambda e: e.activation(T[rg][:], T.rtt[:].indirect(T[eu][:, 48:64]), AF.Copy), ["rtt", eu], [rg])
        gather(h, s, 0)
        gather(h, s, 1)
        op("t", [lambda e: e.matmul(T[pd][:, 0:256], T.idb[:], T[rg][:], True, False),
                 lambda e: e.matmul(T[pd][:, 0:256], T.idn[:], T[fr][:, f0 + 768:f0 + 1024], False, True)],
           ["idb", "idn", rg, "fr%s_%db" % (h, s - 1)], [pd])
        fw = "fw%d" % t
        lo = 64 * int(h)
        op("t", [lambda e: e.matmul(T[kp][:, 0:64], T.idb[:], T[fw][:, lo:lo + 64], True, False),
                 lambda e: e.matmul(T[kp][:, 0:64], T.idb[:], T[fw][:, 128 + lo:128 + lo + 64], False, False)], ["idb", fw], [kp])
        for b in (0, 1):
            Sc(lambda e, b=b: e.activation(T[ab][:, b, :], T[dr][:, 256 * b:256 * b + 256], AF.Abs), [dr + "c%d" % b], [ab + str(b)], 0.3)

    def end(h, s):
        dr, ab, kp, pd = "dr" + h, "ab" + h, "kp" + h, "pd" + h
        gather(h, s, 2)
        Sc(lambda e: e.activation(T[ab][:, 3, :], T[pd][:, 0:256], AF.Abs), [pd], [ab + "3"], 0.3)
        Sc(lambda e: e.activation(T[ab][:, 2, :], T[dr][:, 512:768], AF.Abs), [dr + "c2"], [ab + "2"], 0.3)
        op("t", [lambda e, y=y: e.matmul(T[kp][:, 0:64], T.sel[:, y, :], T[ab][:, :, y * 16:y * 16 + 16], False, y == 15)
                 for y in range(16)], SELK + [ab + "0", ab + "1", ab + "2", ab + "3"], [kp], dur=0.75)

    def L(name):
        i = LNAMES.index(name)
        return T.lists[:, 4 * i:4 * i + 3]

    def close(t):
        EQK = ["eq"] + ["eq%d" % d for d in range(1, 6)]
        for d in range(1, 6):
            V(lambda e, d=d: e.tensor_tensor(T.eq[:, 48 * (d - 1):40 * d], T.hx[:, 1, 8 * d:48], T.hx[:, 1, 0:48 - 8 * d], A.is_equal),
              HXB + ["eq"], ["eq%d" % d])
        V(lambda e: e.tensor_scalar(T.prf[:], T.hx[:, 1, :].indirect(L("ROUT")), 1.0, None, A.add), HXB + ["lists"], ["prf"], 0.11)
        V(lambda e: e.tensor_tensor(T.m1[:], T.eq[:, 0:80], T.eq[:, 80:160], A.max), EQK, ["m1"])
        V(lambda e: e.tensor_tensor(T.m1[:, 0:40], T.m1[:, 0:40], T.m1[:, 40:80], A.max), ["m1"], ["m1"])
        V(lambda e: e.tensor_copy(T.ctf[:], T.hx[:, 0, :].indirect(L("FWD8"))), HXA + ["hx5", "lists"], ["ctf"], 0.11)
        V(lambda e: e.tensor_tensor(T.c48[:, 8:48], T.m1[:, 0:40], T.eq[:, 160:200], A.max), ["m1", "c48"] + EQK, ["c48"])
        V(lambda e: e.tensor_scalar(T.kr[:], T.hx[:, 1, :].indirect(L("ROUT")), -31.0, None, A.add), HXB + ["lists"], ["kr"], 0.11)
        V(lambda e: e.tensor_copy(T.cf[:], T.c48[:].indirect(L("FWD"))), ["c48", "lists"], ["cf"], 0.11)
        V(lambda e: e.tensor_scalar(T.d6[:, 8:48], T.sch[:, :, 15::16], 15, None, A.arith_shift_right),
          ["sch%d%s" % (s, h) for s in range(1, 6) for h in "01"], ["d6"])
        V(lambda e: e.tensor_tensor_scan(T.cc[:], T.segm[:], T.cf[:], 0.0, A.mult, A.max), ["segm", "cf"], ["cc"])
        V(lambda e: e.tensor_tensor(T.ad[:], T.d6[:, 8:48], T.d6[:, 0:40], A.add), ["d6", "d60"], ["ad"])
        V(lambda e: e.tensor_tensor(T.cl[:, 1:48], T.cc[:, 1:48], T.cc[:, 0:47], A.is_gt), ["cc", "cl"], ["cl"])
        V(lambda e: e.tensor_tensor(T.cd[:, 1:48], T.cc[:, 0:47], T.dum[:, 1:48], A.mult), ["cc", "dum", "cd"], ["cd"])
        V(lambda e: e.tensor_tensor_scan(T.cs[:], T.segm[:], T.cc[:], 0.0, A.mult, A.add), ["segm", "cc"], ["cs"])
        V(lambda e: e.tensor_tensor(T.cpr[:], T.cl[:].indirect(L("REV")), T.prf[:], A.mult), ["cl", "prf", "lists"], ["cpr"], 0.11)
        V(lambda e: e.tensor_tensor(T.so[:], T.cd[:], T.ctf[:], A.max), ["cd", "ctf"], ["so"])
        V(lambda e: e.tensor_tensor(T.fs[:], T.fb[:], T.cs[:, 4::6], A.subtract), ["fb", "cs"], ["fs"])
        V(lambda e: e.tensor_tensor_scan(T.bv[:], T.segm[:], T.cpr[:], 0.0, A.mult, A.add), ["segm", "cpr"], ["bv"])
        V(lambda e: e.tensor_copy(T.soff[:], T.so[:].indirect(L("TRS"))), ["so", "lists"], ["soff"], 0.11)
        V(lambda e: e.tensor_scalar(T.fl[:], T.fs[:], 1024.0, None, A.mult), ["fs"], ["fl"])
        for h in "01":
            lo = 64 * int(h)
            Sc(lambda e, h=h, lo=lo: e.activation(T.fout[:, lo:lo + 64], T["fr" + h][:].indirect(T.fl[:, 4 * int(h):4 * int(h) + 4]), AF.Copy),
               ["fl"] + ["fr%s_%d%s" % (h, s, x) for s in range(5) for x in "ab"] + ["fr%s_5_%d" % (h, b) for b in range(4)], ["fout" + h])
        if t < VI - 1:
            dst = T.cores[(rank + 1) % N]
            rid, pid = topo.addr(dst, core)
            send(lambda e: e.remote_dma(T["fin%d" % (t + 1)][:], T.fout[:], T.sem["rf%d" % (t + 1)], T.sem.lsend, pid, rid,
                                        topo.mask(core, dst)), ["fout0", "fout1"], "lsend", len(topo.engines(core, dst)))
        else:
            op("y", lambda e: e.dma_start(T.yf[:], T.fout[:]), ["fout0", "fout1"], ["yf"], "oyf", 16)
        Sc(lambda e: e.activation(T.eall[:], T.tab[:].indirect(T.soff[:, 0:40]), AF.Copy), TABK + ["soff"], ["eall"], dur=0.86)
        V(lambda e: e.tensor_scalar(T.cl2[:], T.cl[:].indirect(L("REV")), 2.0, None, A.mult), ["cl", "lists"], ["cl2"], 0.11)
        V(lambda e: e.tensor_tensor(T.eqv[:], T.bv[:], T.prf[:], A.is_equal), ["bv", "prf"], ["eqv"])
        V(lambda e: e.tensor_tensor(T.cle[:], T.cl[:].indirect(L("REV")), T.eoc[:], A.mult), ["cl", "eoc", "lists"], ["cle"], 0.11)
        V(lambda e: e.tensor_tensor_scan(T.ss[:], T.cl2[:], T.eqv[:], 0.0, A.add, A.subtract), ["cl2", "eqv"], ["ss"])
        if t > 0:
            V(lambda e: e.tensor_scalar(T.ad[:], T.ad[:], T.zc[:, 0:1], None, A.add), ["ad", "zc"], ["ad"])
        V(lambda e: e.tensor_tensor(T.cod[:], T.ss[:], T.kr[:], A.mult), ["ss", "kr"], ["cod"])
        V(lambda e: e.tensor_tensor_scan(T.scb[:], T.segm[:], T.cle[:], 0.0, A.mult, A.add), ["segm", "cle"], ["scb"])
        V(lambda e: e.tensor_scalar(T.cdl[:], T.cod[:].indirect(L("TRL")), 31.0, None, A.add), ["cod", "lists"], ["cdl"], 0.11)
        Sc(lambda e: e.activation(T.hit[:], T.w1[:].indirect(T.cdl[:, 0:40]), AF.Copy), ["w1", "cdl"], ["hit"], dur=0.86)
        V(lambda e: e.tensor_scalar(T.pri[:, 0:40], T.ad[:], 1, None, A.bitwise_and), ["ad", "pri"], ["pri"])
        V(lambda e: e.tensor_tensor(T.sc2[:], T.scb[:], T.eoc[:], A.subtract), ["scb", "eoc"], ["sc2"])
        V(lambda e: e.tensor_tensor(T.fv[:, 0:47], T.ss[:, 0:47], T.ss[:, 1:48], A.is_gt), ["ss", "fv"], ["fv"])
        V(lambda e: e.tensor_tensor(T.sc2[:], T.pri[:].indirect(L("PRR")), T.sc2[:], A.mult), ["pri", "sc2", "lists"], ["sc2"], 0.11)
        V(lambda e: e.tensor_tensor(T.sc2[:], T.sc2[:], T.eoc[:], A.add), ["sc2", "eoc"], ["sc2"])
        V(lambda e: e.tensor_tensor(T.sc2[:], T.sc2[:], T.fv[:], A.mult), ["sc2", "fv"], ["sc2"])
        V(lambda e: e.tensor_tensor_scan(T.tot[:], T.segm[:], T.sc2[:], 0.0, A.mult, A.add), ["segm", "sc2"], ["tot"])
        V(lambda e: e.tensor_copy(T.dec[:], T.tot[:, 5::6]), ["tot"], ["dec"])
        Sc(lambda e: e.activation(T.edec[:], T.eall[:].indirect(T.dec[:]), AF.Copy), ["eall", "dec"], ["edec"], dur=0.22)
        V(lambda e: e.tensor_tensor(T.aa[:], T.w1c[:].indirect(T.cdl[:, 0:40]), T.eall[:], A.mult), ["w1c", "cdl", "eall"], ["aa"], dur=0.85)
        V(lambda e: e.tensor_tensor(T.edec[:], T.aa[:].indirect(T.dec[:]), T.edec[:], A.subtract), ["aa", "dec", "edec"], ["edec"], dur=0.21)
        op("t", lambda e: e.matmul(T.pnew[:, 0:128], T.bon[:], T.edec[:], True, True), ["bon", "edec"], ["pnew"], dur=0.4)
        if t < VI - 1:
            V(lambda e: e.tensor_reduce(T.zr[:], T.cc[:, 5::6], AxisListType.X, A.add), ["cc"], ["zr"])
            op("t", lambda e: e.matmul(T.pmis[:, 0:1], T.onef[:], T.zr[:], True, True), ["onef", "zr"], ["pmis"])
            start_keys(t + 1)
        for r in range(5):
            V(lambda e, r=r: e.tensor_tensor(T.bb[:, 128 * r:128 * r + 128], T.pnew[:, 0:128], T.hit[:, 128 * r:128 * r + 128], A.mult),
              ["pnew", "hit"], ["bb%d" % r], dur=0.11)
        V(lambda e: e.tensor_tensor(T.tab[:].indirect(T.soff[:, 0:40]), T.aa[:], T.bb[:], A.add),
          ["aa", "soff"] + TABK + ["bb%d" % r for r in range(5)], ["tab"], dur=2.0)

    start_keys(0)
    for t in range(VI):
        fin = "fin%d" % t
        start_facts("0", t)
        start_facts("1", t)
        op("t", [lambda e, y=y: e.matmul(T.pmis[:, 8:16], T.sel[:, y, :], T[fin][:, y::16], y == 0, y == 15) for y in range(16)],
           SELK + [fin], ["pmis"])
        spread("0", 0)
        entries("0")
        begin("0", 1, t)
        entries("1")
        end("0", 1)
        spread("1", 0)
        begin("1", 1, t)
        V(lambda e: e.tensor_scalar(T.d6[:, 0:8], T.pmis[:, 8:16], 1.0 / 32768.0, None, A.mult), ["pmis"], ["d60"])
        if t == 1:
            V(lambda e: e.tensor_copy(T.zc[:], T.pmis[:, 0:1]), ["pmis"], ["zc"])
        elif t == 2:
            V(lambda e: e.tensor_tensor(T.zc[:], T.pmis[:, 0:1], T.zc[:], A.add), ["pmis", "zc"], ["zc"])
        if t == 0:
            n = 4 * len(LISTS)
            V(lambda e: e.tensor_tensor(T.lc[:, 0:n], T.la[:, 0:n], T.lb[:, 0:n], A.add),
              [x % i for x in ("la%d", "lb%d") for i in range(len(LISTS))], ["lc"])
            Sc(lambda e: e.activation(T.eoc[:], T.eoi[:], AF.Identity, bias=T.ylf[:, 0:1]), ["eoi", "ylf"], ["eoc"])
            Sc(lambda e: e.activation(T.dum[:], T.dui[:], AF.Identity, bias=T.ylf[:, 0:1]), ["dui", "ylf"], ["dum"])
            Sc(lambda e: e.activation(T.w1c[:], T.w1[:], AF.Copy, scale=-1.0, bias=1.0), ["w1"], ["w1c"])
            Sc(lambda e: e.activation(T.bon[:], T.bof[:], AF.Copy, scale=-1.0), ["bof"], ["bon"])
            V(lambda e: e.tensor_copy(T.lists[:, 0:n], T.lc[:, 0:n]), ["lc"], ["lists"])
        for s in range(1, S + 1):
            collect[0] = s == S
            post("0", s)
            end("1", s)
            if s < S:
                entries("0")
                spread("0", s)
                begin("0", s + 1, t)
            post("1", s)
            if s < S:
                end("0", s + 1)
                entries("1")
                spread("1", s)
                begin("1", s + 1, t)
        close(t)
        collect[0] = False
        schedule()

    for i in range(4):
        pd, o = "pd%d" % (i % 2), 256 * i
        Sc(lambda e: e.activation(T[pd][:, 0:256], T.tab[:, 1024 + o:1280 + o], AF.Copy, scale=4096.0), TABK, [pd])
        V(lambda e: e.tensor_tensor(T.ypt[:, o:o + 256], T[pd][:, 0:256], T.tab[:, o:o + 256], A.add), [pd] + TABK, ["ypt%d" % i])
        op("y", lambda e: e.dma_start(T.yp[:, o:o + 256], T.ypt[:, o:o + 256]), ["ypt%d" % i], ["yp%d" % i], "oyp%d" % i, 16)
    finish()
